import numpy as np
import ml_dtypes


def mxq(x, axis, fmt="e4m3"):
    dtype, down = {"e4m3": (ml_dtypes.float8_e4m3fn, 7), "e5m2": (ml_dtypes.float8_e5m2, 14)}[fmt]
    v = np.moveaxis(np.asarray(x, np.float32).astype(ml_dtypes.bfloat16).astype(np.float64), axis, -1)
    blocks = v.reshape(v.shape[:-1] + (-1, 32))
    amax = np.abs(blocks).max(-1, keepdims=True)
    byte = np.maximum(np.where(amax > 0, np.frexp(amax)[1] - 1 + 127, 0) - down, 1)
    scale = np.exp2(byte - 127.0)
    codes = (blocks / scale).astype(np.float32).astype(dtype).astype(np.float64)
    return np.moveaxis((codes * scale).reshape(v.shape), -1, axis)


WIDE = False


def mx_kscale(k):
    if not WIDE:
        return np.ones(k)
    levels = np.array([10, -10, 5, -5, 0])
    if k % 512:
        return np.exp2(np.random.permutation(np.resize(levels, k // 32))).repeat(32)
    a = np.empty((k // 512, 16))
    for p in range(k // 512):
        a[p, :8] = np.random.permutation(np.resize(levels, 8))
        for g in range(8):
            far = levels[np.abs(levels - a[p, g]) >= 10]
            a[p, g + 8] = far[np.random.randint(len(far))]
    return np.exp2(a.ravel()).repeat(32)


def f64(x):
    return np.asarray(x).astype(np.float64)


def striped(idx):
    return np.tile(idx.reshape(-1, 16).T, (8, 1)).astype(np.uint16)


def unstriped(offs):
    return offs[:16].T.reshape(-1).astype(np.int64)


E2M1 = np.array([0.0, 0.5, 1.0, 1.5, 2.0, 3.0, 4.0, 6.0, -0.0, -0.5, -1.0, -1.5, -2.0, -3.0, -4.0, -6.0])


def pack_weight(w, fmt):
    k, n = w.shape
    w = f64(np.asarray(w, np.float32).astype(ml_dtypes.bfloat16)).reshape(k // 32, 32, n)
    amax = np.abs(w).max(1)
    if fmt == "e4m3":
        byte = np.frexp(amax)[1] - 1 + 127 - 7
    else:
        mant, ex = np.frexp(amax / 6.0)
        byte = np.where(mant > 0.5, ex, ex - 1) + 127
    byte = np.clip(np.where(amax > 0, byte, 1), 1, 254)
    scaled = (w * np.exp2(127.0 - byte)[:, None, :]).reshape(k, n).astype(np.float32)
    by_word = np.ascontiguousarray(scaled.reshape(k // 512, 128, 4, n).transpose(0, 1, 3, 2))
    if fmt == "e4m3":
        words = by_word.astype(ml_dtypes.float8_e4m3fn).view(np.uint8)
    else:
        c = by_word.astype(ml_dtypes.float4_e2m1fn).view(np.uint8) & 0xF
        words = (c[..., 0::2] | (c[..., 1::2] << 4)).reshape(k // 512, 128, 2 * n)
    return np.ascontiguousarray(words), np.ascontiguousarray(byte.astype(np.uint8).reshape(k // 512, 16, n))


def unpack_weight(words, scales, fmt):
    g, _, n = scales.shape
    words = np.ascontiguousarray(words).reshape(g, 128, n, -1)
    if fmt == "e4m3":
        vals = words.view(ml_dtypes.float8_e4m3fn).astype(np.float64)
    else:
        nib = np.empty((g, 128, n, 4), np.uint8)
        nib[..., 0::2] = words & 0xF
        nib[..., 1::2] = words >> 4
        vals = E2M1[nib]
    vals = vals * np.repeat(np.exp2(scales.astype(np.float64) - 127.0), 8, axis=1)[..., None]
    return vals.transpose(0, 1, 3, 2).reshape(g * 512, n)


def relu(v):
    return np.maximum(v, 0.0)


K, T, E, C, H, N = 512, 2048, 4, 256, 512, 384


def by_expert(wq, xq):
    return np.concatenate([wq[e].T @ xq[:, e * C:(e + 1) * C] for e in range(E)], axis=1)


def setup_inputs():
    n = np.random.standard_normal
    s = mx_kscale(K)[:, None]
    u = mx_kscale(H)
    w1 = [pack_weight(m, "e2m1") for m in n((E, K, H)) / np.sqrt(K) / s[None]]
    w3 = [pack_weight(m, "e2m1") for m in n((E, K, H)) / np.sqrt(K) / s[None] * u[None, None, :]]
    w2 = [pack_weight(m, "e2m1") for m in n((E, H, N)) / np.sqrt(H) / u[None, :, None]]
    x = pack_weight(n((K, T)) * s, "e4m3")
    return {
        "x_words": x[0],
        "x_scales": x[1],
        "xr": n((N, T)).astype(np.float32),
        "w1_words": np.stack([m[0] for m in w1]),
        "w1_scales": np.stack([m[1] for m in w1]),
        "w3_words": np.stack([m[0] for m in w3]),
        "w3_scales": np.stack([m[1] for m in w3]),
        "w2_words": np.stack([m[0] for m in w2]),
        "w2_scales": np.stack([m[1] for m in w2]),
        "gate": np.tile(np.random.uniform(0.2, 1.0, E * C), (N, 1)).astype(np.float32),
        "offs": striped(np.random.permutation(T)[:E * C]),
    }


def reference(x_words, x_scales, xr, w1_words, w1_scales, w3_words, w3_scales, w2_words, w2_scales, gate, offs):
    idx = unstriped(offs)
    w1 = np.stack([unpack_weight(w1_words[e], w1_scales[e], "e2m1") for e in range(E)])
    w3 = np.stack([unpack_weight(w3_words[e], w3_scales[e], "e2m1") for e in range(E)])
    w2 = np.stack([unpack_weight(w2_words[e], w2_scales[e], "e2m1") for e in range(E)])
    xq = unpack_weight(x_words, x_scales, "e4m3")[:, idx]
    h = relu(by_expert(w1, xq))
    h = h * by_expert(w3, xq)
    y = by_expert(w2, mxq(h, 0, "e4m3"))
    out = f64(xr).copy()
    out[:, idx] += f64(gate) * y
    return out

@@ -1,0 +1,233 @@
+from contextlib import ExitStack
+
+import concourse.mybir as mybir
+from concourse.masks import make_identity
+
+K, T, E, C, H, N = 512, 2048, 4, 256, 512, 384
+S = E * C
+P = 128
+BANK = 512
+LIST_ROWS = 16
+
+FLOPS = 2 * S * (2 * K * H + H * N)
+
+F32 = mybir.dt.float32
+BF16 = mybir.dt.bfloat16
+I32 = mybir.dt.int32
+U32 = mybir.dt.uint32
+U16 = mybir.dt.uint16
+U8 = mybir.dt.uint8
+FP8X4 = mybir.dt.float8_e4m3fn_x4
+FP4X4 = mybir.dt.float4_e2m1fn_x4
+MULT = mybir.AluOpType.mult
+ADD = mybir.AluOpType.add
+RELU = mybir.ActivationFunctionType.Relu
+
+
+def load_scale_rows(nc, plane, scales, groups):
+    rows = scales.bitcast(I32)
+    dst = plane[:].bitcast(I32)
+    for r in range(4):
+        nc.sync.dma_start(
+            out=dst[r:P:32, :].rearrange("q (g c) -> q g c", g=groups),
+            in_=rows[:, r:16:4, :].rearrange("g q c -> q g c"),
+        )
+
+
+def tile_moe_res_glu_relu_kernel(
+    tc, x_words, x_scales, xr, w1_words, w1_scales, w3_words, w3_scales, w2_words, w2_scales, gate, offs, out
+):
+    nc = tc.nc
+    with ExitStack() as ctx:
+        held = ctx.enter_context(tc.tile_pool(name="held", bufs=1))
+        shared = ctx.enter_context(tc.tile_pool(name="shared", bufs=1))
+        ring = ctx.enter_context(tc.tile_pool(name="ring", bufs=3))
+        psum = ctx.enter_context(tc.psum_pool(name="psum", bufs=2))
+
+        offsets = held.tile([P, S // LIST_ROWS], U16, name="offsets")
+        w1_plane = held.tile([P, E * H], U8, name="w1_plane", align_bytes=64)
+        w3_plane = held.tile([P, E * H], U8, name="w3_plane", align_bytes=64)
+        w2_plane = held.tile([P, E * N], U8, name="w2_plane", align_bytes=64)
+        ident = held.tile([P, P], F32, name="ident")
+        windows = [held.tile([P, T], F32, name="window%d" % i) for i in range(2)]
+
+        ROW = 4 * T
+        x_tile = shared.tile([P, T], I32, name="x_tile", offset=0)
+        w1_tile = shared.tile([P, E * 2 * H], U8, name="w1_tile", offset=ROW, align_bytes=64)
+        w3_tile = shared.tile([P, E * 2 * H], U8, name="w3_tile", offset=ROW + E * 2 * H, align_bytes=64)
+        x_plane = shared.tile([P, T], U8, name="x_plane", offset=2 * ROW, align_bytes=64)
+
+        nc.vector.memset(x_plane[:].bitcast(I32), 0)
+        nc.sync.dma_start(out=x_tile[:], in_=x_words.rearrange("o p t r -> p (o t r)").bitcast(I32))
+        nc.sync.dma_start(offsets[:], offs)
+        load_scale_rows(nc, x_plane, x_scales, 1)
+        nc.vector.memset(w1_plane[:].bitcast(I32), 0)
+        nc.vector.memset(w3_plane[:].bitcast(I32), 0)
+        nc.vector.memset(w2_plane[:].bitcast(I32), 0)
+        for words, scales, w_tile, plane in (
+            (w1_words, w1_scales, w1_tile, w1_plane),
+            (w3_words, w3_scales, w3_tile, w3_plane),
+        ):
+            nc.sync.dma_start(
+                out=w_tile[:].bitcast(I32).rearrange("p (e c) -> p e c", e=E),
+                in_=words.bitcast(I32).rearrange("e s p c -> p (e s) c"),
+            )
+            load_scale_rows(nc, plane, scales.rearrange("e s q c -> (e s) q c"), E)
+        nc.vector.memset(windows[0][:].bitcast(I32), 0)
+        make_identity(nc, ident[:])
+        warm = held.tile([P, 1], F32, name="warm")
+        nc.scalar.activation(warm[:], ident[:, 0:1], RELU)
+        nc.scalar.copy(windows[1][:], windows[0][:])
+
+        def slots_list(first, count):
+            return offsets[:, first // LIST_ROWS : (first + count) // LIST_ROWS]
+
+        slot_words = held.tile([P, S], U32, name="slot_words", align_bytes=64)
+        nc.vector.tensor_copy(slot_words[:], x_tile[:].bitcast(U32).indirect(offsets[:]))
+        first_bytes = held.tile([P, C], U8, name="first_bytes", align_bytes=64)
+        later_bytes = held.tile([P, S - C], U8, name="later_bytes", align_bytes=64)
+        nc.vector.tensor_copy(first_bytes[:], x_plane[:].indirect(slots_list(0, C)))
+        nc.vector.tensor_copy(later_bytes[:], x_plane[:].indirect(slots_list(C, S - C)))
+        xg = [slot_words[:, e * C : (e + 1) * C] for e in range(E)]
+        sg = [first_bytes[:]] + [later_bytes[:, e * C : (e + 1) * C] for e in range(E - 1)]
+
+        gate_tile = shared.tile([P, S], F32, name="gate_tile", offset=0)
+        w2_tile = shared.tile([P, E * 2 * N], U8, name="w2_tile", offset=4 * S, align_bytes=64)
+        nc.sync.dma_start(
+            out=w2_tile[:].bitcast(I32).rearrange("p (e c) -> p e c", e=E),
+            in_=w2_words.bitcast(I32).rearrange("e s p c -> p (e s) c"),
+        )
+        load_scale_rows(nc, w2_plane, w2_scales.rearrange("e s q c -> (e s) q c"), E)
+        nc.sync.dma_start(out=gate_tile[:], in_=gate[0:P, :])
+
+        y_sb = [held.tile([P, S], F32, name="y%d" % b) for b in range(N // P)]
+        hq, hs = [], []
+
+        def first_layer(e):
+            turned = psum.tile([P, BANK], F32, name="turned", tag="turned")
+            for half in range(C // P):
+                cols = slice(half * P, (half + 1) * P)
+                banks = []
+                for w_tile, plane in ((w1_tile, w1_plane), (w3_tile, w3_plane)):
+                    bank = psum.tile([P, BANK], F32, name="wide", tag="wide", bufs=4)
+                    nc.tensor.matmul_mx(
+                        out=bank[:],
+                        lhsT=xg[e][:, cols].bitcast(FP8X4),
+                        lhsT_scale=sg[e][:, cols],
+                        rhs=w_tile[:, e * 2 * H : (e + 1) * 2 * H].bitcast(FP4X4),
+                        rhs_scale=plane[:, e * H : (e + 1) * H],
+                        start=True,
+                        stop=True,
+                    )
+                    banks.append(bank)
+                relu_a = ring.tile([P, H], F32, name="relu_a")
+                nc.scalar.activation(
+                    relu_a[:].rearrange("s (u p d) -> s u p d", u=2, d=2),
+                    banks[0][:].rearrange("s (p u d) -> s u p d", u=2, d=2),
+                    RELU,
+                )
+                h = ring.tile([P, H], BF16, name="h")
+                nc.vector.tensor_tensor(
+                    h[:].rearrange("s (u p d) -> s u p d", u=2, d=2),
+                    banks[1][:].rearrange("s (p u d) -> s u p d", u=2, d=2),
+                    relu_a[:].rearrange("s (u p d) -> s u p d", u=2, d=2),
+                    MULT,
+                )
+                pairs = h[:].bitcast(F32)
+                for u in range(2):
+                    at = (2 * half + u) * P
+                    nc.tensor.transpose(turned[:, at : at + P], pairs[:, u * P : (u + 1) * P], ident[:])
+            grouped = ring.tile([P, 4 * C], BF16, name="grouped", align_bytes=64)
+            nc.scalar.copy(
+                grouped[:].bitcast(F32).rearrange("p (f s u) -> p f s u", f=2, u=2),
+                turned[:].rearrange("p (f u s) -> p f s u", f=2, u=2),
+            )
+            codes = held.tile([P, C], U32, name="hq%d" % e, align_bytes=64)
+            scales = held.tile([P, C], U8, name="hs%d" % e, align_bytes=64)
+            nc.vector.quantize_mx(out=codes[:].bitcast(FP8X4), scales=scales[:], in_=grouped[:])
+            hq.append(codes)
+            hs.append(scales)
+
+        def second_layer(e, b, bank_cols):
+            col = e * N + b * P
+            nc.tensor.matmul_mx(
+                out=bank_cols,
+                lhsT=w2_tile[:, 2 * col : 2 * (col + P)].bitcast(FP4X4),
+                lhsT_scale=w2_plane[:, col : col + P],
+                rhs=hq[e][:].bitcast(FP8X4),
+                rhs_scale=hs[e][:],
+                start=True,
+                stop=True,
+            )
+
+        def scatter(window, b, first, count):
+            nc.vector.tensor_tensor(
+                window[:].indirect(slots_list(first, count)),
+                y_sb[b][:, first : first + count],
+                gate_tile[:, first : first + count],
+                MULT,
+            )
+
+        for e in range(E):
+            first_layer(e)
+            y_bank = psum.tile([P, BANK], F32, name="y_bank", tag="y_bank")
+            second_layer(e, 0, y_bank[:, 0:C])
+            nc.scalar.copy(y_sb[0][:, e * C : (e + 1) * C], y_bank[:, 0:C])
+            scatter(windows[0], 0, e * C, C)
+
+        def load_residual(b, at):
+            xr_tile = shared.tile([P, T], F32, name="xr%d" % b, offset=at)
+            nc.sync.dma_start(out=xr_tile[:], in_=xr[b * P : (b + 1) * P, :])
+            return xr_tile
+
+        def later_block(b, window):
+            for pair in range(E // 2):
+                y_bank = psum.tile([P, BANK], F32, name="y_bank", tag="y_bank")
+                for i in range(2):
+                    second_layer(2 * pair + i, b, y_bank[:, i * C : (i + 1) * C])
+                nc.scalar.copy(y_sb[b][:, pair * BANK : (pair + 1) * BANK], y_bank[:])
+            scatter(window, b, 0, S)
+
+        def add_on_tensor(b, window, xr_tile):
+            sums = []
+            for c in range(T // BANK):
+                summed = psum.tile([P, BANK], F32, name="wide", tag="wide", bufs=4)
+                for j in range(BANK // P):
+                    cols = slice(c * BANK + j * P, c * BANK + (j + 1) * P)
+                    nc.tensor.matmul(
+                        summed[:, j * P : (j + 1) * P], xr_tile[:, cols], ident[:], start=(j == 0), stop=False, is_transpose=True
+                    )
+                sums.append(summed)
+            for c in range(T // BANK):
+                for j in range(BANK // P):
+                    cols = slice(c * BANK + j * P, c * BANK + (j + 1) * P)
+                    nc.tensor.matmul(
+                        sums[c][:, j * P : (j + 1) * P],
+                        window[:, cols],
+                        ident[:],
+                        start=False,
+                        stop=(j == BANK // P - 1),
+                        is_transpose=True,
+                    )
+            for c in range(T // BANK):
+                by_token = ring.tile([P, BANK], F32, name="by_token")
+                nc.scalar.copy(by_token[:], sums[c][:])
+                back = psum.tile([P, BANK], F32, name="turned", tag="turned")
+                for j in range(BANK // P):
+                    nc.tensor.transpose(back[:, j * P : (j + 1) * P], by_token[:, j * P : (j + 1) * P], ident[:])
+                result = ring.tile([P, BANK], F32, name="result")
+                nc.scalar.copy(result[:], back[:])
+                nc.scalar.dma_start(out=out[b * P : (b + 1) * P, c * BANK : (c + 1) * BANK], in_=result[:])
+
+        xr0 = load_residual(0, ROW)
+        xr1 = load_residual(1, 2 * ROW)
+        later_block(1, windows[1])
+        add_on_tensor(0, windows[0], xr0)
+        xr2 = load_residual(2, ROW)
+        later_block(2, windows[0])
+        add_on_tensor(1, windows[1], xr1)
+        for c in range(T // BANK):
+            cols = slice(c * BANK, (c + 1) * BANK)
+            total = ring.tile([P, BANK], F32, name="total", bufs=4)
+            nc.vector.tensor_tensor(total[:], windows[0][:, cols], xr2[:, cols], ADD)
+            nc.sync.dma_start(out=out[2 * P : 3 * P, cols], in_=total[:])

@@ -42,7 +42,7 @@ def tile_moe_res_glu_relu_kernel(
         held = ctx.enter_context(tc.tile_pool(name="held", bufs=1))
         shared = ctx.enter_context(tc.tile_pool(name="shared", bufs=1))
         ring = ctx.enter_context(tc.tile_pool(name="ring", bufs=3))
-        psum = ctx.enter_context(tc.psum_pool(name="psum", bufs=2))
+        psum = ctx.enter_context(tc.psum_pool(name="psum", bufs=1))
 
         offsets = held.tile([P, S // LIST_ROWS], U16, name="offsets")
         w1_plane = held.tile([P, E * H], U8, name="w1_plane", align_bytes=64)
@@ -52,27 +52,30 @@ def tile_moe_res_glu_relu_kernel(
         windows = [held.tile([P, T], F32, name="window%d" % i) for i in range(2)]
 
         ROW = 4 * T
+        HALF = E // 2
         x_tile = shared.tile([P, T], I32, name="x_tile", offset=0)
-        w1_tile = shared.tile([P, E * 2 * H], U8, name="w1_tile", offset=ROW, align_bytes=64)
-        w3_tile = shared.tile([P, E * 2 * H], U8, name="w3_tile", offset=ROW + E * 2 * H, align_bytes=64)
-        x_plane = shared.tile([P, T], U8, name="x_plane", offset=2 * ROW, align_bytes=64)
+        x_plane = shared.tile([P, T], U8, name="x_plane", offset=ROW + T, align_bytes=64)
+
+        def load_words(words, half, w_tile):
+            nc.sync.dma_start(
+                out=w_tile[:].bitcast(I32).rearrange("p (e c) -> p e c", e=HALF),
+                in_=words.bitcast(I32).rearrange("e s p c -> p (e s) c")[:, half * HALF : (half + 1) * HALF, :],
+            )
+
+        w1_tiles = [shared.tile([P, HALF * 2 * H], U8, name="w1_early", offset=2 * ROW, align_bytes=64)]
+        w3_tiles = [shared.tile([P, HALF * 2 * H], U8, name="w3_early", offset=2 * ROW + 2048, align_bytes=64)]
 
         nc.vector.memset(x_plane[:].bitcast(I32), 0)
         nc.sync.dma_start(out=x_tile[:], in_=x_words.rearrange("o p t r -> p (o t r)").bitcast(I32))
         nc.sync.dma_start(offsets[:], offs)
         load_scale_rows(nc, x_plane, x_scales, 1)
-        nc.vector.memset(w1_plane[:].bitcast(I32), 0)
         nc.vector.memset(w3_plane[:].bitcast(I32), 0)
+        nc.vector.memset(w1_plane[:].bitcast(I32), 0)
         nc.vector.memset(w2_plane[:].bitcast(I32), 0)
-        for words, scales, w_tile, plane in (
-            (w1_words, w1_scales, w1_tile, w1_plane),
-            (w3_words, w3_scales, w3_tile, w3_plane),
-        ):
-            nc.sync.dma_start(
-                out=w_tile[:].bitcast(I32).rearrange("p (e c) -> p e c", e=E),
-                in_=words.bitcast(I32).rearrange("e s p c -> p (e s) c"),
-            )
-            load_scale_rows(nc, plane, scales.rearrange("e s q c -> (e s) q c"), E)
+        load_words(w3_words, 0, w3_tiles[0])
+        load_words(w1_words, 0, w1_tiles[0])
+        load_scale_rows(nc, w3_plane, w3_scales.rearrange("e s q c -> (e s) q c"), E)
+        load_scale_rows(nc, w1_plane, w1_scales.rearrange("e s q c -> (e s) q c"), E)
         nc.vector.memset(windows[0][:].bitcast(I32), 0)
         make_identity(nc, ident[:])
         warm = held.tile([P, 1], F32, name="warm")
@@ -82,7 +85,7 @@ def tile_moe_res_glu_relu_kernel(
         def slots_list(first, count):
             return offsets[:, first // LIST_ROWS : (first + count) // LIST_ROWS]
 
-        slot_words = held.tile([P, S], U32, name="slot_words", align_bytes=64)
+        slot_words = shared.tile([P, S], U32, name="slot_words", offset=3 * ROW, align_bytes=64)
         nc.vector.tensor_copy(slot_words[:], x_tile[:].bitcast(U32).indirect(offsets[:]))
         first_bytes = held.tile([P, C], U8, name="first_bytes", align_bytes=64)
         later_bytes = held.tile([P, S - C], U8, name="later_bytes", align_bytes=64)
@@ -91,8 +94,12 @@ def tile_moe_res_glu_relu_kernel(
         xg = [slot_words[:, e * C : (e + 1) * C] for e in range(E)]
         sg = [first_bytes[:]] + [later_bytes[:, e * C : (e + 1) * C] for e in range(E - 1)]
 
-        gate_tile = shared.tile([P, S], F32, name="gate_tile", offset=0)
-        w2_tile = shared.tile([P, E * 2 * N], U8, name="w2_tile", offset=4 * S, align_bytes=64)
+        w1_tiles.append(shared.tile([P, HALF * 2 * H], U8, name="w1_late", offset=0, align_bytes=64))
+        w3_tiles.append(shared.tile([P, HALF * 2 * H], U8, name="w3_late", offset=2048, align_bytes=64))
+        load_words(w1_words, 1, w1_tiles[1])
+        load_words(w3_words, 1, w3_tiles[1])
+        w2_tile = shared.tile([P, E * 2 * N], U8, name="w2_tile", offset=ROW, align_bytes=64)
+        gate_tile = shared.tile([P, S], F32, name="gate_tile", offset=ROW + E * 2 * N)
         nc.sync.dma_start(
             out=w2_tile[:].bitcast(I32).rearrange("p (e c) -> p e c", e=E),
             in_=w2_words.bitcast(I32).rearrange("e s p c -> p (e s) c"),
@@ -103,44 +110,48 @@ def tile_moe_res_glu_relu_kernel(
         y_sb = [held.tile([P, S], F32, name="y%d" % b) for b in range(N // P)]
         hq, hs = [], []
 
-        def first_layer(e):
-            turned = psum.tile([P, BANK], F32, name="turned", tag="turned")
-            for half in range(C // P):
-                cols = slice(half * P, (half + 1) * P)
-                banks = []
-                for w_tile, plane in ((w1_tile, w1_plane), (w3_tile, w3_plane)):
-                    bank = psum.tile([P, BANK], F32, name="wide", tag="wide", bufs=4)
-                    nc.tensor.matmul_mx(
-                        out=bank[:],
-                        lhsT=xg[e][:, cols].bitcast(FP8X4),
-                        lhsT_scale=sg[e][:, cols],
-                        rhs=w_tile[:, e * 2 * H : (e + 1) * 2 * H].bitcast(FP4X4),
-                        rhs_scale=plane[:, e * H : (e + 1) * H],
-                        start=True,
-                        stop=True,
-                    )
-                    banks.append(bank)
-                relu_a = ring.tile([P, H], F32, name="relu_a")
-                nc.scalar.activation(
-                    relu_a[:].rearrange("s (u p d) -> s u p d", u=2, d=2),
-                    banks[0][:].rearrange("s (p u d) -> s u p d", u=2, d=2),
-                    RELU,
+        def bank_tile(number):
+            return psum.tile([P, BANK], F32, name="bank%d" % number, tag="bank%d" % number)
+
+        def stage_tile(number, shape, dtype):
+            return held.tile(shape, dtype, name="stage%d" % number, tag="stage%d" % number, align_bytes=64)
+
+        gated_banks = (0, 1, 3, 1, 3, 1, 3, 1)
+        linear_banks = (2, 0, 2, 0, 2, 0, 4, 0)
+        turned = {}
+
+        def first_layer(i):
+            e, half = divmod(i, C // P)
+            if half == 0:
+                turned[e] = bank_tile(5 + e % 2)
+            cols = slice(half * P, (half + 1) * P)
+            banks = []
+            for w_tiles, plane, number in ((w1_tiles, w1_plane, gated_banks[i]), (w3_tiles, w3_plane, linear_banks[i])):
+                bank = bank_tile(number)
+                nc.tensor.matmul_mx(
+                    out=bank[:],
+                    lhsT=xg[e][:, cols].bitcast(FP8X4),
+                    lhsT_scale=sg[e][:, cols],
+                    rhs=w_tiles[e // HALF][:, (e % HALF) * 2 * H : (e % HALF + 1) * 2 * H].bitcast(FP4X4),
+                    rhs_scale=plane[:, e * H : (e + 1) * H],
+                    start=True,
+                    stop=True,
                 )
-                h = ring.tile([P, H], BF16, name="h")
-                nc.vector.tensor_tensor(
-                    h[:].rearrange("s (u p d) -> s u p d", u=2, d=2),
-                    banks[1][:].rearrange("s (p u d) -> s u p d", u=2, d=2),
-                    relu_a[:].rearrange("s (u p d) -> s u p d", u=2, d=2),
-                    MULT,
-                )
-                pairs = h[:].bitcast(F32)
-                for u in range(2):
-                    at = (2 * half + u) * P
-                    nc.tensor.transpose(turned[:, at : at + P], pairs[:, u * P : (u + 1) * P], ident[:])
-            grouped = ring.tile([P, 4 * C], BF16, name="grouped", align_bytes=64)
+                banks.append(bank)
+            relu_a = stage_tile(i % 4, [P, H], F32)
+            nc.scalar.activation(relu_a[:], banks[0][:], RELU)
+            h = ring.tile([P, H], BF16, name="h")
+            nc.vector.tensor_tensor(h[:], banks[1][:], relu_a[:], MULT)
+            pairs = h[:].bitcast(F32)
+            for u in range(2):
+                at = (2 * half + u) * P
+                nc.tensor.transpose(turned[e][:, at : at + P], pairs[:, u : 2 * P : 2], ident[:])
+
+        def quantise(e, stage):
+            grouped = stage_tile(stage, [P, 4 * C], BF16)
             nc.scalar.copy(
                 grouped[:].bitcast(F32).rearrange("p (f s u) -> p f s u", f=2, u=2),
-                turned[:].rearrange("p (f u s) -> p f s u", f=2, u=2),
+                turned[e][:].rearrange("p (f u s) -> p f s u", f=2, u=2),
             )
             codes = held.tile([P, C], U32, name="hq%d" % e, align_bytes=64)
             scales = held.tile([P, C], U8, name="hs%d" % e, align_bytes=64)
@@ -168,30 +179,40 @@ def tile_moe_res_glu_relu_kernel(
                 MULT,
             )
 
-        for e in range(E):
-            first_layer(e)
-            y_bank = psum.tile([P, BANK], F32, name="y_bank", tag="y_bank")
-            second_layer(e, 0, y_bank[:, 0:C])
-            nc.scalar.copy(y_sb[0][:, e * C : (e + 1) * C], y_bank[:, 0:C])
+        def results(b, experts, number):
+            bank = bank_tile(number)
+            for i, e in enumerate(experts):
+                second_layer(e, b, bank[:, i * C : (i + 1) * C])
+            nc.scalar.copy(y_sb[b][:, experts[0] * C : (experts[-1] + 1) * C], bank[:, 0 : len(experts) * C])
+
+        def first_block(e, number):
+            results(0, [e], number)
             scatter(windows[0], 0, e * C, C)
+
+        for i in range(4):
+            first_layer(i)
+        quantise(0, 2)
+        first_layer(4)
+        first_layer(5)
+        quantise(1, 0)
+        first_block(0, 2)
+        first_layer(6)
+        first_layer(7)
+        quantise(2, 2)
+        first_block(1, 4)
+        quantise(3, 1)
+        first_block(2, 0)
+        first_block(3, 2)
 
         def load_residual(b, at):
             xr_tile = shared.tile([P, T], F32, name="xr%d" % b, offset=at)
             nc.sync.dma_start(out=xr_tile[:], in_=xr[b * P : (b + 1) * P, :])
             return xr_tile
 
-        def later_block(b, window):
-            for pair in range(E // 2):
-                y_bank = psum.tile([P, BANK], F32, name="y_bank", tag="y_bank")
-                for i in range(2):
-                    second_layer(2 * pair + i, b, y_bank[:, i * C : (i + 1) * C])
-                nc.scalar.copy(y_sb[b][:, pair * BANK : (pair + 1) * BANK], y_bank[:])
-            scatter(window, b, 0, S)
-
-        def add_on_tensor(b, window, xr_tile):
+        def add_on_tensor(b, window, xr_tile, numbers):
             sums = []
             for c in range(T // BANK):
-                summed = psum.tile([P, BANK], F32, name="wide", tag="wide", bufs=4)
+                summed = bank_tile(numbers[c])
                 for j in range(BANK // P):
                     cols = slice(c * BANK + j * P, c * BANK + (j + 1) * P)
                     nc.tensor.matmul(
@@ -212,20 +233,26 @@ def tile_moe_res_glu_relu_kernel(
             for c in range(T // BANK):
                 by_token = ring.tile([P, BANK], F32, name="by_token")
                 nc.scalar.copy(by_token[:], sums[c][:])
-                back = psum.tile([P, BANK], F32, name="turned", tag="turned")
+                back = bank_tile((7, 5)[c % 2])
                 for j in range(BANK // P):
                     nc.tensor.transpose(back[:, j * P : (j + 1) * P], by_token[:, j * P : (j + 1) * P], ident[:])
-                result = ring.tile([P, BANK], F32, name="result")
-                nc.scalar.copy(result[:], back[:])
-                nc.scalar.dma_start(out=out[b * P : (b + 1) * P, c * BANK : (c + 1) * BANK], in_=result[:])
+                if c % 2 == 0:
+                    result = ring.tile([P, 2 * BANK], F32, name="result", bufs=2)
+                nc.scalar.copy(result[:, (c % 2) * BANK : (c % 2 + 1) * BANK], back[:])
+                if c % 2 == 1:
+                    nc.scalar.dma_start(out=out[b * P : (b + 1) * P, (c - 1) * BANK : (c + 1) * BANK], in_=result[:])
 
-        xr0 = load_residual(0, ROW)
-        xr1 = load_residual(1, 2 * ROW)
-        later_block(1, windows[1])
-        add_on_tensor(0, windows[0], xr0)
-        xr2 = load_residual(2, ROW)
-        later_block(2, windows[0])
-        add_on_tensor(1, windows[1], xr1)
+        xr0 = load_residual(0, 2 * ROW)
+        xr1 = load_residual(1, 3 * ROW)
+        results(1, [0, 1], 5)
+        results(1, [2, 3], 7)
+        scatter(windows[1], 1, 0, S)
+        results(2, [0, 1], 6)
+        results(2, [2, 3], 5)
+        add_on_tensor(0, windows[0], xr0, (3, 1, 4, 0))
+        xr2 = load_residual(2, 2 * ROW)
+        scatter(windows[0], 2, 0, S)
+        add_on_tensor(1, windows[1], xr1, (2, 6, 3, 1))
         for c in range(T // BANK):
             cols = slice(c * BANK, (c + 1) * BANK)
             total = ring.tile([P, BANK], F32, name="total", bufs=4)

@@ -8,8 +8,13 @@ S = E * C
 P = 128
 BANK = 512
 LIST_ROWS = 16
+SCALE_ROWS = 16
+QUADRANT = 32
+HALF = E // 2
+ROW = 4 * T
 
 FLOPS = 2 * S * (2 * K * H + H * N)
+BYTES = K * T + K * T // 32 + E * (2 * K * H + H * N) * 17 // 32 + 4 * S + 2 * P * S // LIST_ROWS + 2 * 4 * N * T
 
 F32 = mybir.dt.float32
 BF16 = mybir.dt.bfloat16
@@ -22,6 +27,13 @@ FP4X4 = mybir.dt.float4_e2m1fn_x4
 MULT = mybir.AluOpType.mult
 ADD = mybir.AluOpType.add
 RELU = mybir.ActivationFunctionType.Relu
+COPY = mybir.ActivationFunctionType.Copy
+
+W1_BANKS = (0, 1, 3, 1, 3, 1, 3, 1)
+W3_BANKS = (2, 0, 2, 0, 2, 0, 4, 0)
+TURN_BANKS = (5, 6)
+SPARE_BANK = 7
+STAGES = 4
 
 
 def load_scale_rows(nc, plane, scales, groups):
@@ -29,8 +41,8 @@ def load_scale_rows(nc, plane, scales, groups):
     dst = plane[:].bitcast(I32)
     for r in range(4):
         nc.sync.dma_start(
-            out=dst[r:P:32, :].rearrange("q (g c) -> q g c", g=groups),
-            in_=rows[:, r:16:4, :].rearrange("g q c -> q g c"),
+            out=dst[r:P:QUADRANT, :].rearrange("q (g c) -> q g c", g=groups),
+            in_=rows[:, r:SCALE_ROWS:4, :].rearrange("g q c -> q g c"),
         )
 
 
@@ -51,10 +63,10 @@ def tile_moe_res_glu_relu_kernel(
         ident = held.tile([P, P], F32, name="ident")
         windows = [held.tile([P, T], F32, name="window%d" % i) for i in range(2)]
 
-        ROW = 4 * T
-        HALF = E // 2
         x_tile = shared.tile([P, T], I32, name="x_tile", offset=0)
         x_plane = shared.tile([P, T], U8, name="x_plane", offset=ROW + T, align_bytes=64)
+
+        half_bytes = HALF * 2 * H
 
         def load_words(words, half, w_tile):
             nc.sync.dma_start(
@@ -62,8 +74,8 @@ def tile_moe_res_glu_relu_kernel(
                 in_=words.bitcast(I32).rearrange("e s p c -> p (e s) c")[:, half * HALF : (half + 1) * HALF, :],
             )
 
-        w1_tiles = [shared.tile([P, HALF * 2 * H], U8, name="w1_early", offset=2 * ROW, align_bytes=64)]
-        w3_tiles = [shared.tile([P, HALF * 2 * H], U8, name="w3_early", offset=2 * ROW + 2048, align_bytes=64)]
+        w1_tiles = [shared.tile([P, half_bytes], U8, name="w1_early", offset=2 * ROW, align_bytes=64)]
+        w3_tiles = [shared.tile([P, half_bytes], U8, name="w3_early", offset=2 * ROW + half_bytes, align_bytes=64)]
 
         nc.vector.memset(x_plane[:].bitcast(I32), 0)
         nc.sync.dma_start(out=x_tile[:], in_=x_words.rearrange("o p t r -> p (o t r)").bitcast(I32))
@@ -76,26 +88,25 @@ def tile_moe_res_glu_relu_kernel(
         load_words(w1_words, 0, w1_tiles[0])
         load_scale_rows(nc, w3_plane, w3_scales.rearrange("e s q c -> (e s) q c"), E)
         load_scale_rows(nc, w1_plane, w1_scales.rearrange("e s q c -> (e s) q c"), E)
+
         nc.vector.memset(windows[0][:].bitcast(I32), 0)
         make_identity(nc, ident[:])
-        warm = held.tile([P, 1], F32, name="warm")
-        nc.scalar.activation(warm[:], ident[:, 0:1], RELU)
-        nc.scalar.copy(windows[1][:], windows[0][:])
+        nc.scalar.activation(windows[1][:], windows[0][:], COPY)
 
-        def slots_list(first, count):
+        def slot_offsets(first, count):
             return offsets[:, first // LIST_ROWS : (first + count) // LIST_ROWS]
 
         slot_words = shared.tile([P, S], U32, name="slot_words", offset=3 * ROW, align_bytes=64)
         nc.vector.tensor_copy(slot_words[:], x_tile[:].bitcast(U32).indirect(offsets[:]))
         first_bytes = held.tile([P, C], U8, name="first_bytes", align_bytes=64)
         later_bytes = held.tile([P, S - C], U8, name="later_bytes", align_bytes=64)
-        nc.vector.tensor_copy(first_bytes[:], x_plane[:].indirect(slots_list(0, C)))
-        nc.vector.tensor_copy(later_bytes[:], x_plane[:].indirect(slots_list(C, S - C)))
-        xg = [slot_words[:, e * C : (e + 1) * C] for e in range(E)]
-        sg = [first_bytes[:]] + [later_bytes[:, e * C : (e + 1) * C] for e in range(E - 1)]
+        nc.vector.tensor_copy(first_bytes[:], x_plane[:].indirect(slot_offsets(0, C)))
+        nc.vector.tensor_copy(later_bytes[:], x_plane[:].indirect(slot_offsets(C, S - C)))
+        expert_words = [slot_words[:, e * C : (e + 1) * C] for e in range(E)]
+        expert_bytes = [first_bytes[:]] + [later_bytes[:, e * C : (e + 1) * C] for e in range(E - 1)]
 
-        w1_tiles.append(shared.tile([P, HALF * 2 * H], U8, name="w1_late", offset=0, align_bytes=64))
-        w3_tiles.append(shared.tile([P, HALF * 2 * H], U8, name="w3_late", offset=2048, align_bytes=64))
+        w1_tiles.append(shared.tile([P, half_bytes], U8, name="w1_late", offset=0, align_bytes=64))
+        w3_tiles.append(shared.tile([P, half_bytes], U8, name="w3_late", offset=half_bytes, align_bytes=64))
         load_words(w1_words, 1, w1_tiles[1])
         load_words(w3_words, 1, w3_tiles[1])
         w2_tile = shared.tile([P, E * 2 * N], U8, name="w2_tile", offset=ROW, align_bytes=64)
@@ -107,8 +118,9 @@ def tile_moe_res_glu_relu_kernel(
         load_scale_rows(nc, w2_plane, w2_scales.rearrange("e s q c -> (e s) q c"), E)
         nc.sync.dma_start(out=gate_tile[:], in_=gate[0:P, :])
 
-        y_sb = [held.tile([P, S], F32, name="y%d" % b) for b in range(N // P)]
-        hq, hs = [], []
+        y_tiles = [held.tile([P, S], F32, name="y%d" % b) for b in range(N // P)]
+        h_codes, h_scales = [], []
+        turned = {}
 
         def bank_tile(number):
             return psum.tile([P, BANK], F32, name="bank%d" % number, tag="bank%d" % number)
@@ -116,29 +128,25 @@ def tile_moe_res_glu_relu_kernel(
         def stage_tile(number, shape, dtype):
             return held.tile(shape, dtype, name="stage%d" % number, tag="stage%d" % number, align_bytes=64)
 
-        gated_banks = (0, 1, 3, 1, 3, 1, 3, 1)
-        linear_banks = (2, 0, 2, 0, 2, 0, 4, 0)
-        turned = {}
-
-        def first_layer(i):
-            e, half = divmod(i, C // P)
+        def first_layer(tile):
+            e, half = divmod(tile, C // P)
             if half == 0:
-                turned[e] = bank_tile(5 + e % 2)
+                turned[e] = bank_tile(TURN_BANKS[e % 2])
             cols = slice(half * P, (half + 1) * P)
             banks = []
-            for w_tiles, plane, number in ((w1_tiles, w1_plane, gated_banks[i]), (w3_tiles, w3_plane, linear_banks[i])):
+            for w_tiles, plane, number in ((w1_tiles, w1_plane, W1_BANKS[tile]), (w3_tiles, w3_plane, W3_BANKS[tile])):
                 bank = bank_tile(number)
                 nc.tensor.matmul_mx(
                     out=bank[:],
-                    lhsT=xg[e][:, cols].bitcast(FP8X4),
-                    lhsT_scale=sg[e][:, cols],
+                    lhsT=expert_words[e][:, cols].bitcast(FP8X4),
+                    lhsT_scale=expert_bytes[e][:, cols],
                     rhs=w_tiles[e // HALF][:, (e % HALF) * 2 * H : (e % HALF + 1) * 2 * H].bitcast(FP4X4),
                     rhs_scale=plane[:, e * H : (e + 1) * H],
                     start=True,
                     stop=True,
                 )
                 banks.append(bank)
-            relu_a = stage_tile(i % 4, [P, H], F32)
+            relu_a = stage_tile(tile % STAGES, [P, H], F32)
             nc.scalar.activation(relu_a[:], banks[0][:], RELU)
             h = ring.tile([P, H], BF16, name="h")
             nc.vector.tensor_tensor(h[:], banks[1][:], relu_a[:], MULT)
@@ -156,105 +164,104 @@ def tile_moe_res_glu_relu_kernel(
             codes = held.tile([P, C], U32, name="hq%d" % e, align_bytes=64)
             scales = held.tile([P, C], U8, name="hs%d" % e, align_bytes=64)
             nc.vector.quantize_mx(out=codes[:].bitcast(FP8X4), scales=scales[:], in_=grouped[:])
-            hq.append(codes)
-            hs.append(scales)
+            h_codes.append(codes)
+            h_scales.append(scales)
 
-        def second_layer(e, b, bank_cols):
-            col = e * N + b * P
-            nc.tensor.matmul_mx(
-                out=bank_cols,
-                lhsT=w2_tile[:, 2 * col : 2 * (col + P)].bitcast(FP4X4),
-                lhsT_scale=w2_plane[:, col : col + P],
-                rhs=hq[e][:].bitcast(FP8X4),
-                rhs_scale=hs[e][:],
-                start=True,
-                stop=True,
-            )
+        def second_layer(block, experts, number):
+            bank = bank_tile(number)
+            for place, e in enumerate(experts):
+                col = e * N + block * P
+                nc.tensor.matmul_mx(
+                    out=bank[:, place * C : (place + 1) * C],
+                    lhsT=w2_tile[:, 2 * col : 2 * (col + P)].bitcast(FP4X4),
+                    lhsT_scale=w2_plane[:, col : col + P],
+                    rhs=h_codes[e][:].bitcast(FP8X4),
+                    rhs_scale=h_scales[e][:],
+                    start=True,
+                    stop=True,
+                )
+            nc.scalar.copy(y_tiles[block][:, experts[0] * C : (experts[-1] + 1) * C], bank[:, 0 : len(experts) * C])
 
-        def scatter(window, b, first, count):
+        def scatter(window, block, first, count):
             nc.vector.tensor_tensor(
-                window[:].indirect(slots_list(first, count)),
-                y_sb[b][:, first : first + count],
+                window[:].indirect(slot_offsets(first, count)),
+                y_tiles[block][:, first : first + count],
                 gate_tile[:, first : first + count],
                 MULT,
             )
 
-        def results(b, experts, number):
-            bank = bank_tile(number)
-            for i, e in enumerate(experts):
-                second_layer(e, b, bank[:, i * C : (i + 1) * C])
-            nc.scalar.copy(y_sb[b][:, experts[0] * C : (experts[-1] + 1) * C], bank[:, 0 : len(experts) * C])
-
         def first_block(e, number):
-            results(0, [e], number)
+            second_layer(0, [e], number)
             scatter(windows[0], 0, e * C, C)
 
-        for i in range(4):
-            first_layer(i)
-        quantise(0, 2)
+        for tile in range(4):
+            first_layer(tile)
+        quantise(0, 2 % STAGES)
         first_layer(4)
         first_layer(5)
-        quantise(1, 0)
-        first_block(0, 2)
+        quantise(1, 4 % STAGES)
+        first_block(0, W3_BANKS[4])
         first_layer(6)
         first_layer(7)
-        quantise(2, 2)
-        first_block(1, 4)
-        quantise(3, 1)
-        first_block(2, 0)
-        first_block(3, 2)
+        quantise(2, 6 % STAGES)
+        first_block(1, W3_BANKS[6])
+        quantise(3, 5 % STAGES)
+        first_block(2, W3_BANKS[7])
+        first_block(3, W3_BANKS[4])
 
-        def load_residual(b, at):
-            xr_tile = shared.tile([P, T], F32, name="xr%d" % b, offset=at)
-            nc.sync.dma_start(out=xr_tile[:], in_=xr[b * P : (b + 1) * P, :])
+        def load_residual(block, stretch):
+            xr_tile = shared.tile([P, T], F32, name="xr%d" % block, offset=stretch * ROW)
+            nc.sync.dma_start(out=xr_tile[:], in_=xr[block * P : (block + 1) * P, :])
             return xr_tile
 
-        def add_on_tensor(b, window, xr_tile, numbers):
+        def add_on_tensor(block, window, xr_tile, numbers):
+            per_bank = BANK // P
             sums = []
             for c in range(T // BANK):
                 summed = bank_tile(numbers[c])
-                for j in range(BANK // P):
+                for j in range(per_bank):
                     cols = slice(c * BANK + j * P, c * BANK + (j + 1) * P)
                     nc.tensor.matmul(
                         summed[:, j * P : (j + 1) * P], xr_tile[:, cols], ident[:], start=(j == 0), stop=False, is_transpose=True
                     )
                 sums.append(summed)
             for c in range(T // BANK):
-                for j in range(BANK // P):
+                for j in range(per_bank):
                     cols = slice(c * BANK + j * P, c * BANK + (j + 1) * P)
                     nc.tensor.matmul(
                         sums[c][:, j * P : (j + 1) * P],
                         window[:, cols],
                         ident[:],
                         start=False,
-                        stop=(j == BANK // P - 1),
+                        stop=(j == per_bank - 1),
                         is_transpose=True,
                     )
             for c in range(T // BANK):
                 by_token = ring.tile([P, BANK], F32, name="by_token")
                 nc.scalar.copy(by_token[:], sums[c][:])
-                back = bank_tile((7, 5)[c % 2])
-                for j in range(BANK // P):
+                back = bank_tile((SPARE_BANK, TURN_BANKS[0])[c % 2])
+                for j in range(per_bank):
                     nc.tensor.transpose(back[:, j * P : (j + 1) * P], by_token[:, j * P : (j + 1) * P], ident[:])
                 if c % 2 == 0:
                     result = ring.tile([P, 2 * BANK], F32, name="result", bufs=2)
                 nc.scalar.copy(result[:, (c % 2) * BANK : (c % 2 + 1) * BANK], back[:])
                 if c % 2 == 1:
-                    nc.scalar.dma_start(out=out[b * P : (b + 1) * P, (c - 1) * BANK : (c + 1) * BANK], in_=result[:])
+                    nc.scalar.dma_start(out=out[block * P : (block + 1) * P, (c - 1) * BANK : (c + 1) * BANK], in_=result[:])
 
-        xr0 = load_residual(0, 2 * ROW)
-        xr1 = load_residual(1, 3 * ROW)
-        results(1, [0, 1], 5)
-        results(1, [2, 3], 7)
+        xr0 = load_residual(0, 2)
+        xr1 = load_residual(1, 3)
+        second_layer(1, [0, 1], TURN_BANKS[0])
+        second_layer(1, [2, 3], SPARE_BANK)
         scatter(windows[1], 1, 0, S)
-        results(2, [0, 1], 6)
-        results(2, [2, 3], 5)
-        add_on_tensor(0, windows[0], xr0, (3, 1, 4, 0))
-        xr2 = load_residual(2, 2 * ROW)
+        second_layer(2, [0, 1], TURN_BANKS[1])
+        second_layer(2, [2, 3], TURN_BANKS[0])
+        add_on_tensor(0, windows[0], xr0, (W1_BANKS[6], W1_BANKS[7], W3_BANKS[6], W3_BANKS[7]))
+        xr2 = load_residual(2, 2)
         scatter(windows[0], 2, 0, S)
-        add_on_tensor(1, windows[1], xr1, (2, 6, 3, 1))
+        add_on_tensor(1, windows[1], xr1, (W3_BANKS[4], TURN_BANKS[1], W1_BANKS[6], W1_BANKS[7]))
+
         for c in range(T // BANK):
             cols = slice(c * BANK, (c + 1) * BANK)
-            total = ring.tile([P, BANK], F32, name="total", bufs=4)
+            total = ring.tile([P, BANK], F32, name="total", bufs=T // BANK)
             nc.vector.tensor_tensor(total[:], windows[0][:, cols], xr2[:, cols], ADD)
             nc.sync.dma_start(out=out[2 * P : 3 * P, cols], in_=total[:])

@@ -29,18 +29,17 @@ ADD = mybir.AluOpType.add
 RELU = mybir.ActivationFunctionType.Relu
 COPY = mybir.ActivationFunctionType.Copy
 
-W1_BANKS = (0, 1, 3, 1, 3, 1, 3, 1)
-W3_BANKS = (2, 0, 2, 0, 2, 0, 4, 0)
+A_BANKS = (0, 1, 2, 3, 4, 0, 1, 2)
+B_BANKS = (3, 4, 0, 1, 2, 3, 4, 0)
 TURN_BANKS = (5, 6)
-SPARE_BANK = 7
-STAGES = 4
+PIECE = 512
 
 
-def load_scale_rows(nc, plane, scales, groups):
+def load_scale_rows(queue, plane, scales, groups):
     rows = scales.bitcast(I32)
     dst = plane[:].bitcast(I32)
     for r in range(4):
-        nc.sync.dma_start(
+        queue.dma_start(
             out=dst[r:P:QUADRANT, :].rearrange("q (g c) -> q g c", g=groups),
             in_=rows[:, r:SCALE_ROWS:4, :].rearrange("g q c -> q g c"),
         )
@@ -52,7 +51,6 @@ def tile_moe_res_glu_relu_kernel(
     nc = tc.nc
     with ExitStack() as ctx:
         held = ctx.enter_context(tc.tile_pool(name="held", bufs=1))
-        shared = ctx.enter_context(tc.tile_pool(name="shared", bufs=1))
         ring = ctx.enter_context(tc.tile_pool(name="ring", bufs=3))
         psum = ctx.enter_context(tc.psum_pool(name="psum", bufs=1))
 
@@ -61,12 +59,16 @@ def tile_moe_res_glu_relu_kernel(
         w3_plane = held.tile([P, E * H], U8, name="w3_plane", align_bytes=64)
         w2_plane = held.tile([P, E * N], U8, name="w2_plane", align_bytes=64)
         ident = held.tile([P, P], F32, name="ident")
-        windows = [held.tile([P, T], F32, name="window%d" % i) for i in range(2)]
-
-        x_tile = shared.tile([P, T], I32, name="x_tile", offset=0)
-        x_plane = shared.tile([P, T], U8, name="x_plane", offset=ROW + T, align_bytes=64)
+        windows = [held.tile([P, T], F32, name="window%d" % b) for b in range(N // P)]
 
         half_bytes = HALF * 2 * H
+        x_tile = held.tile([P, T], I32, name="x_tile")
+        x_plane = held.tile([P, T], U8, name="x_plane", align_bytes=64)
+        w1_tiles = [held.tile([P, half_bytes], U8, name="w1_%d" % i, align_bytes=64) for i in range(2)]
+        w3_tiles = [held.tile([P, half_bytes], U8, name="w3_%d" % i, align_bytes=64) for i in range(2)]
+        w2_tile = held.tile([P, E * 2 * N], U8, name="w2_tile", align_bytes=64)
+        gate_tile = held.tile([P, S], F32, name="gate_tile")
+        xr_tiles = [held.tile([P, T], F32, name="xr%d" % b) for b in range(N // P)]
 
         def load_words(words, half, w_tile):
             nc.sync.dma_start(
@@ -74,89 +76,113 @@ def tile_moe_res_glu_relu_kernel(
                 in_=words.bitcast(I32).rearrange("e s p c -> p (e s) c")[:, half * HALF : (half + 1) * HALF, :],
             )
 
-        w1_tiles = [shared.tile([P, half_bytes], U8, name="w1_early", offset=2 * ROW, align_bytes=64)]
-        w3_tiles = [shared.tile([P, half_bytes], U8, name="w3_early", offset=2 * ROW + half_bytes, align_bytes=64)]
+        def load_gate(first, end):
+            nc.sync.dma_start(out=gate_tile[:, first:end], in_=gate[0:P, first:end])
+
+        def load_residual(b):
+            nc.sync.dma_start(out=xr_tiles[b][:], in_=xr[b * P : (b + 1) * P, :])
 
         nc.vector.memset(x_plane[:].bitcast(I32), 0)
-        nc.sync.dma_start(out=x_tile[:], in_=x_words.rearrange("o p t r -> p (o t r)").bitcast(I32))
-        nc.sync.dma_start(offsets[:], offs)
-        load_scale_rows(nc, x_plane, x_scales, 1)
-        nc.vector.memset(w3_plane[:].bitcast(I32), 0)
+        nc.vector.memset(windows[0][:, 0:BANK].bitcast(I32), 0)
         nc.vector.memset(w1_plane[:].bitcast(I32), 0)
+        nc.vector.memset(w3_plane[:].bitcast(I32), 0)
         nc.vector.memset(w2_plane[:].bitcast(I32), 0)
-        load_words(w3_words, 0, w3_tiles[0])
-        load_words(w1_words, 0, w1_tiles[0])
-        load_scale_rows(nc, w3_plane, w3_scales.rearrange("e s q c -> (e s) q c"), E)
-        load_scale_rows(nc, w1_plane, w1_scales.rearrange("e s q c -> (e s) q c"), E)
-
-        nc.vector.memset(windows[0][:].bitcast(I32), 0)
+        nc.vector.memset(windows[0][:, BANK:T].bitcast(I32), 0)
         make_identity(nc, ident[:])
-        nc.scalar.activation(windows[1][:], windows[0][:], COPY)
+        zeros = windows[0][:, 0:BANK].unsqueeze(1).to_broadcast([P, T // BANK, BANK])
+        for window in windows[1:]:
+            nc.scalar.activation(window[:].rearrange("p (a c) -> p a c", c=BANK), zeros, COPY)
 
-        def slot_offsets(first, count):
-            return offsets[:, first // LIST_ROWS : (first + count) // LIST_ROWS]
-
-        slot_words = shared.tile([P, S], U32, name="slot_words", offset=3 * ROW, align_bytes=64)
-        nc.vector.tensor_copy(slot_words[:], x_tile[:].bitcast(U32).indirect(offsets[:]))
-        first_bytes = held.tile([P, C], U8, name="first_bytes", align_bytes=64)
-        later_bytes = held.tile([P, S - C], U8, name="later_bytes", align_bytes=64)
-        nc.vector.tensor_copy(first_bytes[:], x_plane[:].indirect(slot_offsets(0, C)))
-        nc.vector.tensor_copy(later_bytes[:], x_plane[:].indirect(slot_offsets(C, S - C)))
-        expert_words = [slot_words[:, e * C : (e + 1) * C] for e in range(E)]
-        expert_bytes = [first_bytes[:]] + [later_bytes[:, e * C : (e + 1) * C] for e in range(E - 1)]
-
-        w1_tiles.append(shared.tile([P, half_bytes], U8, name="w1_late", offset=0, align_bytes=64))
-        w3_tiles.append(shared.tile([P, half_bytes], U8, name="w3_late", offset=half_bytes, align_bytes=64))
+        nc.sync.dma_start(offsets[:], offs)
+        load_words(w1_words, 0, w1_tiles[0])
+        load_scale_rows(nc.sync, x_plane, x_scales, 1)
+        nc.sync.dma_start(out=x_tile[:], in_=x_words.rearrange("o p t r -> p (o t r)").bitcast(I32))
+        load_scale_rows(nc.sync, w1_plane, w1_scales.rearrange("e s q c -> (e s) q c"), E)
+        load_words(w3_words, 0, w3_tiles[0])
+        load_scale_rows(nc.sync, w3_plane, w3_scales.rearrange("e s q c -> (e s) q c"), E)
         load_words(w1_words, 1, w1_tiles[1])
         load_words(w3_words, 1, w3_tiles[1])
-        w2_tile = shared.tile([P, E * 2 * N], U8, name="w2_tile", offset=ROW, align_bytes=64)
-        gate_tile = shared.tile([P, S], F32, name="gate_tile", offset=ROW + E * 2 * N)
+        load_scale_rows(nc.sync, w2_plane, w2_scales.rearrange("e s q c -> (e s) q c"), E)
         nc.sync.dma_start(
             out=w2_tile[:].bitcast(I32).rearrange("p (e c) -> p e c", e=E),
             in_=w2_words.bitcast(I32).rearrange("e s p c -> p (e s) c"),
         )
-        load_scale_rows(nc, w2_plane, w2_scales.rearrange("e s q c -> (e s) q c"), E)
-        nc.sync.dma_start(out=gate_tile[:], in_=gate[0:P, :])
+        load_gate(0, S // 2)
+        load_gate(S // 2, S)
+        load_residual(1)
+        load_residual(0)
+        load_residual(2)
 
-        y_tiles = [held.tile([P, S], F32, name="y%d" % b) for b in range(N // P)]
+        def slot_offsets(first, count):
+            return offsets[:, first // LIST_ROWS : (first + count) // LIST_ROWS]
+
+        slot_bytes = held.tile([P, S], U8, name="slot_bytes", align_bytes=64)
+        nc.vector.tensor_copy(slot_bytes[:], x_plane[:].indirect(offsets[:]))
+        expert_words = []
+        for first, count in ((0, 1), (1, 1), (2, 2)):
+            part = held.tile([P, count * C], U32, name="words%d" % first, align_bytes=64)
+            nc.vector.tensor_copy(part[:], x_tile[:].bitcast(U32).indirect(slot_offsets(first * C, count * C)))
+            expert_words.extend(part[:, i * C : (i + 1) * C] for i in range(count))
+        expert_bytes = [slot_bytes[:, e * C : (e + 1) * C] for e in range(E)]
+
         h_codes, h_scales = [], []
         turned = {}
+        relus = {}
+        b_banks = {}
 
         def bank_tile(number):
             return psum.tile([P, BANK], F32, name="bank%d" % number, tag="bank%d" % number)
 
-        def stage_tile(number, shape, dtype):
-            return held.tile(shape, dtype, name="stage%d" % number, tag="stage%d" % number, align_bytes=64)
-
-        def first_layer(tile):
+        def product(tile, w_tiles, plane, number):
             e, half = divmod(tile, C // P)
+            cols = slice(half * P, (half + 1) * P)
+            bank = bank_tile(number)
+            nc.tensor.matmul_mx(
+                out=bank[:],
+                lhsT=expert_words[e][:, cols].bitcast(FP8X4),
+                lhsT_scale=expert_bytes[e][:, cols],
+                rhs=w_tiles[e // HALF][:, (e % HALF) * 2 * H : (e % HALF + 1) * 2 * H].bitcast(FP4X4),
+                rhs_scale=plane[:, e * H : (e + 1) * H],
+                start=True,
+                stop=True,
+            )
+            return bank
+
+        a_banks = {}
+
+        def product_a(tile):
+            a_banks[tile] = product(tile, w1_tiles, w1_plane, A_BANKS[tile])
+
+        def product_b(tile):
+            b_banks[tile] = product(tile, w3_tiles, w3_plane, B_BANKS[tile])
+
+        def by_pairs(bank):
+            return bank[:].rearrange("s (p u d) -> s u p d", u=2, d=2)
+
+        def relu(tile):
+            relus[tile] = held.tile([P, H], F32, name="relu%d" % tile)
+            nc.scalar.activation(
+                relus[tile][:].rearrange("s (u p d) -> s u p d", u=2, d=2), by_pairs(a_banks[tile]), RELU
+            )
+
+        def hidden(tile):
+            e, half = divmod(tile, C // P)
+            h = ring.tile([P, H], BF16, name="h")
+            nc.vector.tensor_tensor(
+                h[:].rearrange("s (u p d) -> s u p d", u=2, d=2),
+                by_pairs(b_banks[tile]),
+                relus[tile][:].rearrange("s (u p d) -> s u p d", u=2, d=2),
+                MULT,
+            )
             if half == 0:
                 turned[e] = bank_tile(TURN_BANKS[e % 2])
-            cols = slice(half * P, (half + 1) * P)
-            banks = []
-            for w_tiles, plane, number in ((w1_tiles, w1_plane, W1_BANKS[tile]), (w3_tiles, w3_plane, W3_BANKS[tile])):
-                bank = bank_tile(number)
-                nc.tensor.matmul_mx(
-                    out=bank[:],
-                    lhsT=expert_words[e][:, cols].bitcast(FP8X4),
-                    lhsT_scale=expert_bytes[e][:, cols],
-                    rhs=w_tiles[e // HALF][:, (e % HALF) * 2 * H : (e % HALF + 1) * 2 * H].bitcast(FP4X4),
-                    rhs_scale=plane[:, e * H : (e + 1) * H],
-                    start=True,
-                    stop=True,
-                )
-                banks.append(bank)
-            relu_a = stage_tile(tile % STAGES, [P, H], F32)
-            nc.scalar.activation(relu_a[:], banks[0][:], RELU)
-            h = ring.tile([P, H], BF16, name="h")
-            nc.vector.tensor_tensor(h[:], banks[1][:], relu_a[:], MULT)
             pairs = h[:].bitcast(F32)
             for u in range(2):
                 at = (2 * half + u) * P
-                nc.tensor.transpose(turned[e][:, at : at + P], pairs[:, u : 2 * P : 2], ident[:])
+                nc.tensor.transpose(turned[e][:, at : at + P], pairs[:, u * P : (u + 1) * P], ident[:])
 
-        def quantise(e, stage):
-            grouped = stage_tile(stage, [P, 4 * C], BF16)
+        def quantise(e):
+            grouped = held.tile([P, 4 * C], BF16, name="grouped%d" % e, align_bytes=64)
             nc.scalar.copy(
                 grouped[:].bitcast(F32).rearrange("p (f s u) -> p f s u", f=2, u=2),
                 turned[e][:].rearrange("p (f u s) -> p f s u", f=2, u=2),
@@ -167,9 +193,9 @@ def tile_moe_res_glu_relu_kernel(
             h_codes.append(codes)
             h_scales.append(scales)
 
-        def second_layer(block, experts, number):
+        def second_layer(units, number):
             bank = bank_tile(number)
-            for place, e in enumerate(experts):
+            for place, (block, e) in enumerate(units):
                 col = e * N + block * P
                 nc.tensor.matmul_mx(
                     out=bank[:, place * C : (place + 1) * C],
@@ -180,88 +206,71 @@ def tile_moe_res_glu_relu_kernel(
                     start=True,
                     stop=True,
                 )
-            nc.scalar.copy(y_tiles[block][:, experts[0] * C : (experts[-1] + 1) * C], bank[:, 0 : len(experts) * C])
+            return bank
 
-        def scatter(window, block, first, count):
+        gated = held.tile([P, N // P, S], F32, name="gated")
+
+        def gated_experts(block, first, count, number):
+            bank = second_layer([(block, e) for e in range(first, first + count)], number)
+            cols = slice(first * C, (first + count) * C)
+            nc.vector.tensor_tensor(gated[:, block, cols], bank[:, 0 : count * C], gate_tile[:, cols], MULT)
+
+        def gated_blocks(e, first, number):
+            bank = second_layer([(first, e), (first + 1, e)], number)
+            cols = slice(e * C, (e + 1) * C)
             nc.vector.tensor_tensor(
-                window[:].indirect(slot_offsets(first, count)),
-                y_tiles[block][:, first : first + count],
-                gate_tile[:, first : first + count],
+                gated[:, first : first + 2, cols],
+                bank[:].rearrange("p (b c) -> p b c", b=2),
+                gate_tile[:, cols].unsqueeze(1).to_broadcast([P, 2, C]),
                 MULT,
             )
 
-        def first_block(e, number):
-            second_layer(0, [e], number)
-            scatter(windows[0], 0, e * C, C)
+        def scatter_on_scalar(block, first, end):
+            nc.scalar.activation(windows[block][:].indirect(slot_offsets(first, end - first)), gated[:, block, first:end], COPY)
 
-        for tile in range(4):
-            first_layer(tile)
-        quantise(0, 2 % STAGES)
-        first_layer(4)
-        first_layer(5)
-        quantise(1, 4 % STAGES)
-        first_block(0, W3_BANKS[4])
-        first_layer(6)
-        first_layer(7)
-        quantise(2, 6 % STAGES)
-        first_block(1, W3_BANKS[6])
-        quantise(3, 5 % STAGES)
-        first_block(2, W3_BANKS[7])
-        first_block(3, W3_BANKS[4])
+        def scatter_on_vector(block, first, end):
+            nc.vector.tensor_copy(windows[block][:].indirect(slot_offsets(first, end - first)), gated[:, block, first:end])
 
-        def load_residual(block, stretch):
-            xr_tile = shared.tile([P, T], F32, name="xr%d" % block, offset=stretch * ROW)
-            nc.sync.dma_start(out=xr_tile[:], in_=xr[block * P : (block + 1) * P, :])
-            return xr_tile
+        def add_and_store(block):
+            for c in range(T // PIECE):
+                cols = slice(c * PIECE, (c + 1) * PIECE)
+                total = held.tile([P, PIECE], F32, name="total%d_%d" % (block, c))
+                nc.vector.tensor_tensor(total[:], windows[block][:, cols], xr_tiles[block][:, cols], ADD)
+                nc.sync.dma_start(out=out[block * P : (block + 1) * P, cols], in_=total[:])
 
-        def add_on_tensor(block, window, xr_tile, numbers):
-            per_bank = BANK // P
-            sums = []
-            for c in range(T // BANK):
-                summed = bank_tile(numbers[c])
-                for j in range(per_bank):
-                    cols = slice(c * BANK + j * P, c * BANK + (j + 1) * P)
-                    nc.tensor.matmul(
-                        summed[:, j * P : (j + 1) * P], xr_tile[:, cols], ident[:], start=(j == 0), stop=False, is_transpose=True
-                    )
-                sums.append(summed)
-            for c in range(T // BANK):
-                for j in range(per_bank):
-                    cols = slice(c * BANK + j * P, c * BANK + (j + 1) * P)
-                    nc.tensor.matmul(
-                        sums[c][:, j * P : (j + 1) * P],
-                        window[:, cols],
-                        ident[:],
-                        start=False,
-                        stop=(j == per_bank - 1),
-                        is_transpose=True,
-                    )
-            for c in range(T // BANK):
-                by_token = ring.tile([P, BANK], F32, name="by_token")
-                nc.scalar.copy(by_token[:], sums[c][:])
-                back = bank_tile((SPARE_BANK, TURN_BANKS[0])[c % 2])
-                for j in range(per_bank):
-                    nc.tensor.transpose(back[:, j * P : (j + 1) * P], by_token[:, j * P : (j + 1) * P], ident[:])
-                if c % 2 == 0:
-                    result = ring.tile([P, 2 * BANK], F32, name="result", bufs=2)
-                nc.scalar.copy(result[:, (c % 2) * BANK : (c % 2 + 1) * BANK], back[:])
-                if c % 2 == 1:
-                    nc.scalar.dma_start(out=out[block * P : (block + 1) * P, (c - 1) * BANK : (c + 1) * BANK], in_=result[:])
-
-        xr0 = load_residual(0, 2)
-        xr1 = load_residual(1, 3)
-        second_layer(1, [0, 1], TURN_BANKS[0])
-        second_layer(1, [2, 3], SPARE_BANK)
-        scatter(windows[1], 1, 0, S)
-        second_layer(2, [0, 1], TURN_BANKS[1])
-        second_layer(2, [2, 3], TURN_BANKS[0])
-        add_on_tensor(0, windows[0], xr0, (W1_BANKS[6], W1_BANKS[7], W3_BANKS[6], W3_BANKS[7]))
-        xr2 = load_residual(2, 2)
-        scatter(windows[0], 2, 0, S)
-        add_on_tensor(1, windows[1], xr1, (W3_BANKS[4], TURN_BANKS[1], W1_BANKS[6], W1_BANKS[7]))
-
-        for c in range(T // BANK):
-            cols = slice(c * BANK, (c + 1) * BANK)
-            total = ring.tile([P, BANK], F32, name="total", bufs=T // BANK)
-            nc.vector.tensor_tensor(total[:], windows[0][:, cols], xr2[:, cols], ADD)
-            nc.sync.dma_start(out=out[2 * P : 3 * P, cols], in_=total[:])
+        for tile in range(3):
+            product_a(tile)
+        product_b(0)
+        product_b(1)
+        for tile in range(3):
+            relu(tile)
+        for tile in range(8):
+            if tile + 2 < 8:
+                product_b(tile + 2)
+            hidden(tile)
+            if tile + 3 < 8:
+                product_a(tile + 3)
+                relu(tile + 3)
+            if tile in (3, 5):
+                quantise(tile // 2 - 1)
+            if tile == 6:
+                gated_experts(0, 0, 1, A_BANKS[7])
+        quantise(2)
+        scatter_on_scalar(0, 0, C)
+        gated_experts(1, 0, 2, B_BANKS[7])
+        gated_blocks(2, 1, A_BANKS[6])
+        gated_experts(2, 0, 2, B_BANKS[7])
+        quantise(3)
+        scatter_on_scalar(1, 0, 384)
+        gated_experts(0, 1, 2, TURN_BANKS[1])
+        gated_blocks(3, 0, 7)
+        gated_experts(2, 3, 1, B_BANKS[6])
+        scatter_on_vector(2, 0, C)
+        scatter_on_scalar(0, C, 640)
+        scatter_on_scalar(0, 640, S)
+        scatter_on_vector(1, 384, S)
+        scatter_on_scalar(2, C, 640)
+        scatter_on_scalar(2, 640, S)
+        add_and_store(1)
+        add_and_store(0)
+        add_and_store(2)

@@ -29,16 +29,16 @@ ADD = mybir.AluOpType.add
 RELU = mybir.ActivationFunctionType.Relu
 COPY = mybir.ActivationFunctionType.Copy
 
-A_BANKS = (0, 1, 2, 3, 4, 0, 1, 2)
-B_BANKS = (3, 4, 0, 1, 2, 3, 4, 0)
+A_BANKS = (0, 1, 2, 7, 3, 4, 0, 1)
+B_BANKS = (3, 4, 0, 1, 2, 7, 3, 4)
 TURN_BANKS = (5, 6)
 PIECE = 512
 
 
-def load_scale_rows(queue, plane, scales, groups):
+def load_scale_rows(queue, plane, scales, groups, which=range(4)):
     rows = scales.bitcast(I32)
     dst = plane[:].bitcast(I32)
-    for r in range(4):
+    for r in which:
         queue.dma_start(
             out=dst[r:P:QUADRANT, :].rearrange("q (g c) -> q g c", g=groups),
             in_=rows[:, r:SCALE_ROWS:4, :].rearrange("g q c -> q g c"),
@@ -62,13 +62,13 @@ def tile_moe_res_glu_relu_kernel(
         windows = [held.tile([P, T], F32, name="window%d" % b) for b in range(N // P)]
 
         half_bytes = HALF * 2 * H
-        x_tile = held.tile([P, T], I32, name="x_tile")
+        x_tile = held.tile([P, T], I32, name="x_tile", tag="tokens")
         x_plane = held.tile([P, T], U8, name="x_plane", align_bytes=64)
         w1_tiles = [held.tile([P, half_bytes], U8, name="w1_%d" % i, align_bytes=64) for i in range(2)]
         w3_tiles = [held.tile([P, half_bytes], U8, name="w3_%d" % i, align_bytes=64) for i in range(2)]
         w2_tile = held.tile([P, E * 2 * N], U8, name="w2_tile", align_bytes=64)
         gate_tile = held.tile([P, S], F32, name="gate_tile")
-        xr_tiles = [held.tile([P, T], F32, name="xr%d" % b) for b in range(N // P)]
+        xr_tiles = {}
 
         def load_words(words, half, w_tile):
             nc.sync.dma_start(
@@ -76,19 +76,25 @@ def tile_moe_res_glu_relu_kernel(
                 in_=words.bitcast(I32).rearrange("e s p c -> p (e s) c")[:, half * HALF : (half + 1) * HALF, :],
             )
 
+        def load_w2(first, end):
+            nc.sync.dma_start(
+                out=w2_tile[:, first * 2 * N : end * 2 * N].bitcast(I32).rearrange("p (e c) -> p e c", e=end - first),
+                in_=w2_words.bitcast(I32).rearrange("e s p c -> p (e s) c")[:, first:end, :],
+            )
+
         def load_gate(first, end):
             nc.sync.dma_start(out=gate_tile[:, first:end], in_=gate[0:P, first:end])
 
-        def load_residual(b):
+        def load_residual(b, tag):
+            xr_tiles[b] = held.tile([P, T], F32, name="xr%d" % b, tag=tag)
             nc.sync.dma_start(out=xr_tiles[b][:], in_=xr[b * P : (b + 1) * P, :])
 
         nc.vector.memset(x_plane[:].bitcast(I32), 0)
         nc.vector.memset(windows[0][:, 0:BANK].bitcast(I32), 0)
         nc.vector.memset(w1_plane[:].bitcast(I32), 0)
         nc.vector.memset(w3_plane[:].bitcast(I32), 0)
-        nc.vector.memset(w2_plane[:].bitcast(I32), 0)
         nc.vector.memset(windows[0][:, BANK:T].bitcast(I32), 0)
-        make_identity(nc, ident[:])
+        nc.gpsimd.memset(w2_plane[:].bitcast(I32), 0)
         zeros = windows[0][:, 0:BANK].unsqueeze(1).to_broadcast([P, T // BANK, BANK])
         for window in windows[1:]:
             nc.scalar.activation(window[:].rearrange("p (a c) -> p a c", c=BANK), zeros, COPY)
@@ -96,22 +102,20 @@ def tile_moe_res_glu_relu_kernel(
         nc.sync.dma_start(offsets[:], offs)
         load_words(w1_words, 0, w1_tiles[0])
         load_scale_rows(nc.sync, x_plane, x_scales, 1)
+        load_scale_rows(nc.sync, w1_plane, w1_scales.rearrange("e s q c -> (e s) q c"), E, (0,))
         nc.sync.dma_start(out=x_tile[:], in_=x_words.rearrange("o p t r -> p (o t r)").bitcast(I32))
-        load_scale_rows(nc.sync, w1_plane, w1_scales.rearrange("e s q c -> (e s) q c"), E)
         load_words(w3_words, 0, w3_tiles[0])
-        load_scale_rows(nc.sync, w3_plane, w3_scales.rearrange("e s q c -> (e s) q c"), E)
+        load_scale_rows(nc.sync, w3_plane, w3_scales.rearrange("e s q c -> (e s) q c"), E, (0, 1, 2,))
+        load_scale_rows(nc.sync, w1_plane, w1_scales.rearrange("e s q c -> (e s) q c"), E, (1, 2, 3,))
+        load_scale_rows(nc.sync, w3_plane, w3_scales.rearrange("e s q c -> (e s) q c"), E, (3,))
+        load_scale_rows(nc.gpsimd, w2_plane, w2_scales.rearrange("e s q c -> (e s) q c"), E)
+        make_identity(nc, ident[:])
+        load_w2(0, 1)
+        load_gate(0, C)
         load_words(w1_words, 1, w1_tiles[1])
         load_words(w3_words, 1, w3_tiles[1])
-        load_scale_rows(nc.sync, w2_plane, w2_scales.rearrange("e s q c -> (e s) q c"), E)
-        nc.sync.dma_start(
-            out=w2_tile[:].bitcast(I32).rearrange("p (e c) -> p e c", e=E),
-            in_=w2_words.bitcast(I32).rearrange("e s p c -> p (e s) c"),
-        )
-        load_gate(0, S // 2)
-        load_gate(S // 2, S)
-        load_residual(1)
-        load_residual(0)
-        load_residual(2)
+        load_w2(1, E)
+        load_gate(C, S)
 
         def slot_offsets(first, count):
             return offsets[:, first // LIST_ROWS : (first + count) // LIST_ROWS]
@@ -124,6 +128,9 @@ def tile_moe_res_glu_relu_kernel(
             nc.vector.tensor_copy(part[:], x_tile[:].bitcast(U32).indirect(slot_offsets(first * C, count * C)))
             expert_words.extend(part[:, i * C : (i + 1) * C] for i in range(count))
         expert_bytes = [slot_bytes[:, e * C : (e + 1) * C] for e in range(E)]
+        load_residual(1, "tokens")
+        load_residual(0, "xr0")
+        load_residual(2, "xr2")
 
         h_codes, h_scales = [], []
         turned = {}
@@ -165,28 +172,39 @@ def tile_moe_res_glu_relu_kernel(
                 relus[tile][:].rearrange("s (u p d) -> s u p d", u=2, d=2), by_pairs(a_banks[tile]), RELU
             )
 
+        hs = {}
+
         def hidden(tile):
             e, half = divmod(tile, C // P)
-            h = ring.tile([P, H], BF16, name="h")
+            if half == 0:
+                hs[e] = ring.tile([P, 2, H], BF16, name="h")
             nc.vector.tensor_tensor(
-                h[:].rearrange("s (u p d) -> s u p d", u=2, d=2),
+                hs[e][:, half, :].rearrange("s (u p d) -> s u p d", u=2, d=2),
                 by_pairs(b_banks[tile]),
                 relus[tile][:].rearrange("s (u p d) -> s u p d", u=2, d=2),
                 MULT,
             )
-            if half == 0:
-                turned[e] = bank_tile(TURN_BANKS[e % 2])
-            pairs = h[:].bitcast(F32)
-            for u in range(2):
-                at = (2 * half + u) * P
-                nc.tensor.transpose(turned[e][:, at : at + P], pairs[:, u * P : (u + 1) * P], ident[:])
 
-        def quantise(e):
-            grouped = held.tile([P, 4 * C], BF16, name="grouped%d" % e, align_bytes=64)
+        def turn(e):
+            turned[e] = bank_tile(TURN_BANKS[e % 2])
+            pairs = hs[e][:].bitcast(F32)
+            for half in range(2):
+                for u in range(2):
+                    at = (2 * half + u) * P
+                    nc.tensor.transpose(turned[e][:, at : at + P], pairs[:, half, u * P : (u + 1) * P], ident[:])
+
+        groups = {}
+
+        def regroup(e):
+            grouped = held.tile([P, 4 * C], BF16, name="grouped%d" % e, tag="stage%d" % e, align_bytes=64)
+            groups[e] = grouped
             nc.scalar.copy(
                 grouped[:].bitcast(F32).rearrange("p (f s u) -> p f s u", f=2, u=2),
                 turned[e][:].rearrange("p (f u s) -> p f s u", f=2, u=2),
             )
+
+        def quantise(e):
+            grouped = groups[e]
             codes = held.tile([P, C], U32, name="hq%d" % e, align_bytes=64)
             scales = held.tile([P, C], U8, name="hs%d" % e, align_bytes=64)
             nc.vector.quantize_mx(out=codes[:].bitcast(FP8X4), scales=scales[:], in_=grouped[:])
@@ -210,8 +228,12 @@ def tile_moe_res_glu_relu_kernel(
 
         gated = held.tile([P, N // P, S], F32, name="gated")
 
-        def gated_experts(block, first, count, number):
-            bank = second_layer([(block, e) for e in range(first, first + count)], number)
+        def experts_product(block, first, count, number):
+            return second_layer([(block, e) for e in range(first, first + count)], number)
+
+        def gated_experts(block, first, count, number, bank=None):
+            if bank is None:
+                bank = experts_product(block, first, count, number)
             cols = slice(first * C, (first + count) * C)
             nc.vector.tensor_tensor(gated[:, block, cols], bank[:, 0 : count * C], gate_tile[:, cols], MULT)
 
@@ -231,46 +253,72 @@ def tile_moe_res_glu_relu_kernel(
         def scatter_on_vector(block, first, end):
             nc.vector.tensor_copy(windows[block][:].indirect(slot_offsets(first, end - first)), gated[:, block, first:end])
 
-        def add_and_store(block):
-            for c in range(T // PIECE):
-                cols = slice(c * PIECE, (c + 1) * PIECE)
-                total = held.tile([P, PIECE], F32, name="total%d_%d" % (block, c))
-                nc.vector.tensor_tensor(total[:], windows[block][:, cols], xr_tiles[block][:, cols], ADD)
-                nc.sync.dma_start(out=out[block * P : (block + 1) * P, cols], in_=total[:])
+        def add_and_store(engines, block, cuts=(0, 512, 1024, 1536, 2048)):
+            total = held.tile([P, T], F32, name="total%d" % block, tag="xr0" if block == 1 else "total%d" % block)
+            for c in range(len(cuts) - 1):
+                cols = slice(cuts[c], cuts[c + 1])
+                engines[c].tensor_tensor(total[:, cols], windows[block][:, cols], xr_tiles[block][:, cols], ADD)
+                nc.sync.dma_start(out=out[block * P : (block + 1) * P, cols], in_=total[:, cols])
 
-        for tile in range(3):
-            product_a(tile)
+        product_a(0)
+        product_a(1)
+        product_a(2)
         product_b(0)
+        product_a(3)
         product_b(1)
-        for tile in range(3):
-            relu(tile)
-        for tile in range(8):
-            if tile + 2 < 8:
-                product_b(tile + 2)
-            hidden(tile)
-            if tile + 3 < 8:
-                product_a(tile + 3)
-                relu(tile + 3)
-            if tile in (3, 5):
-                quantise(tile // 2 - 1)
-            if tile == 6:
-                gated_experts(0, 0, 1, A_BANKS[7])
+        relu(0)
+        relu(1)
+        product_b(2)
+        relu(2)
+        relu(3)
+        hidden(0)
+        product_a(4)
+        product_b(3)
+        relu(4)
+        hidden(1)
+        turn(0)
+        regroup(0)
+        product_a(5)
+        product_b(4)
+        relu(5)
+        hidden(2)
+        product_a(6)
+        product_b(5)
+        relu(6)
+        hidden(3)
+        turn(1)
+        regroup(1)
+        product_a(7)
+        product_b(6)
+        relu(7)
+        quantise(0)
+        hidden(4)
+        product_b(7)
+        hidden(5)
+        first_bank = experts_product(0, 0, 1, B_BANKS[5])
+        turn(2)
+        regroup(2)
+        quantise(1)
+        hidden(6)
+        first_gated = held.tile([P, C], F32, name="first_gated", tag="stage3", align_bytes=64)
+        nc.vector.tensor_tensor(first_gated[:], first_bank[:, 0:C], gate_tile[:, 0:C], MULT)
+        nc.scalar.activation(windows[0][:].indirect(slot_offsets(0, C)), first_gated[:], COPY)
+        hidden(7)
+        turn(3)
+        regroup(3)
         quantise(2)
-        scatter_on_scalar(0, 0, C)
-        gated_experts(1, 0, 2, B_BANKS[7])
-        gated_blocks(2, 1, A_BANKS[6])
-        gated_experts(2, 0, 2, B_BANKS[7])
-        quantise(3)
-        scatter_on_scalar(1, 0, 384)
-        gated_experts(0, 1, 2, TURN_BANKS[1])
-        gated_blocks(3, 0, 7)
-        gated_experts(2, 3, 1, B_BANKS[6])
-        scatter_on_vector(2, 0, C)
+        gated_experts(0, 1, 2, B_BANKS[6])
         scatter_on_scalar(0, C, 640)
+        gated_experts(1, 0, 2, B_BANKS[7])
+        quantise(3)
+        gated_experts(0, 3, 1, A_BANKS[6])
         scatter_on_scalar(0, 640, S)
-        scatter_on_vector(1, 384, S)
-        scatter_on_scalar(2, C, 640)
-        scatter_on_scalar(2, 640, S)
-        add_and_store(1)
-        add_and_store(0)
-        add_and_store(2)
+        gated_experts(2, 2, 2, TURN_BANKS[0])
+        gated_experts(2, 0, 2, A_BANKS[6])
+        gated_experts(1, 2, 2, TURN_BANKS[0])
+        scatter_on_vector(1, 0, S)
+        for first, end in ((0, 384), (384, 704), (704, S)):
+            scatter_on_scalar(2, first, end)
+        add_and_store([nc.gpsimd] * 4, 0)
+        add_and_store([nc.vector] * 4, 1)
+        add_and_store([nc.vector] * 5, 2, (0, 512, 1024, 1536, 1792, 2048))

@@ -93,8 +93,9 @@ def tile_moe_res_glu_relu_kernel(
         nc.vector.memset(windows[0][:, 0:BANK].bitcast(I32), 0)
         nc.vector.memset(w1_plane[:].bitcast(I32), 0)
         nc.vector.memset(w3_plane[:].bitcast(I32), 0)
+        nc.vector.memset(w2_plane[:].bitcast(I32), 0)
         nc.vector.memset(windows[0][:, BANK:T].bitcast(I32), 0)
-        nc.gpsimd.memset(w2_plane[:].bitcast(I32), 0)
+        make_identity(nc, ident[:])
         zeros = windows[0][:, 0:BANK].unsqueeze(1).to_broadcast([P, T // BANK, BANK])
         for window in windows[1:]:
             nc.scalar.activation(window[:].rearrange("p (a c) -> p a c", c=BANK), zeros, COPY)
@@ -105,15 +106,14 @@ def tile_moe_res_glu_relu_kernel(
         load_scale_rows(nc.sync, w1_plane, w1_scales.rearrange("e s q c -> (e s) q c"), E, (0,))
         nc.sync.dma_start(out=x_tile[:], in_=x_words.rearrange("o p t r -> p (o t r)").bitcast(I32))
         load_words(w3_words, 0, w3_tiles[0])
-        load_scale_rows(nc.sync, w3_plane, w3_scales.rearrange("e s q c -> (e s) q c"), E, (0, 1, 2,))
         load_scale_rows(nc.sync, w1_plane, w1_scales.rearrange("e s q c -> (e s) q c"), E, (1, 2, 3,))
+        load_scale_rows(nc.sync, w3_plane, w3_scales.rearrange("e s q c -> (e s) q c"), E, (0, 1, 2,))
+        load_scale_rows(nc.sync, w2_plane, w2_scales.rearrange("e s q c -> (e s) q c"), E)
+        load_words(w1_words, 1, w1_tiles[1])
         load_scale_rows(nc.sync, w3_plane, w3_scales.rearrange("e s q c -> (e s) q c"), E, (3,))
-        load_scale_rows(nc.gpsimd, w2_plane, w2_scales.rearrange("e s q c -> (e s) q c"), E)
-        make_identity(nc, ident[:])
+        load_words(w3_words, 1, w3_tiles[1])
         load_w2(0, 1)
         load_gate(0, C)
-        load_words(w1_words, 1, w1_tiles[1])
-        load_words(w3_words, 1, w3_tiles[1])
         load_w2(1, E)
         load_gate(C, S)
 
@@ -195,10 +195,10 @@ def tile_moe_res_glu_relu_kernel(
 
         groups = {}
 
-        def regroup(e):
+        def regroup(e, copy):
             grouped = held.tile([P, 4 * C], BF16, name="grouped%d" % e, tag="stage%d" % e, align_bytes=64)
             groups[e] = grouped
-            nc.scalar.copy(
+            copy(
                 grouped[:].bitcast(F32).rearrange("p (f s u) -> p f s u", f=2, u=2),
                 turned[e][:].rearrange("p (f u s) -> p f s u", f=2, u=2),
             )
@@ -260,65 +260,64 @@ def tile_moe_res_glu_relu_kernel(
                 engines[c].tensor_tensor(total[:, cols], windows[block][:, cols], xr_tiles[block][:, cols], ADD)
                 nc.sync.dma_start(out=out[block * P : (block + 1) * P, cols], in_=total[:, cols])
 
-        product_a(0)
-        product_a(1)
-        product_a(2)
+        for tile in range(4):
+            product_a(tile)
         product_b(0)
-        product_a(3)
         product_b(1)
         relu(0)
         relu(1)
         product_b(2)
+        product_b(3)
         relu(2)
         relu(3)
         hidden(0)
         product_a(4)
-        product_b(3)
         relu(4)
         hidden(1)
         turn(0)
-        regroup(0)
         product_a(5)
         product_b(4)
         relu(5)
         hidden(2)
         product_a(6)
         product_b(5)
-        relu(6)
         hidden(3)
         turn(1)
-        regroup(1)
+        regroup(1, nc.scalar.copy)
+        relu(6)
         product_a(7)
         product_b(6)
         relu(7)
-        quantise(0)
+        regroup(0, nc.vector.tensor_copy)
         hidden(4)
         product_b(7)
+        quantise(0)
+        first_bank = experts_product(0, 0, 1, TURN_BANKS[0])
         hidden(5)
-        first_bank = experts_product(0, 0, 1, B_BANKS[5])
+        gated_experts(0, 0, 1, TURN_BANKS[0], first_bank)
+        scatter_on_scalar(0, 0, C)
         turn(2)
-        regroup(2)
+        regroup(2, nc.scalar.copy)
         quantise(1)
         hidden(6)
-        first_gated = held.tile([P, C], F32, name="first_gated", tag="stage3", align_bytes=64)
-        nc.vector.tensor_tensor(first_gated[:], first_bank[:, 0:C], gate_tile[:, 0:C], MULT)
-        nc.scalar.activation(windows[0][:].indirect(slot_offsets(0, C)), first_gated[:], COPY)
         hidden(7)
         turn(3)
-        regroup(3)
+        regroup(3, nc.scalar.copy)
+        gated_blocks(0, 1, B_BANKS[4])
+        gated_experts(0, 1, 1, B_BANKS[7])
+        scatter_on_scalar(0, C, 2 * C)
+        gated_blocks(1, 1, B_BANKS[5])
         quantise(2)
-        gated_experts(0, 1, 2, B_BANKS[6])
-        scatter_on_scalar(0, C, 640)
-        gated_experts(1, 0, 2, B_BANKS[7])
+        gated_experts(0, 2, 1, B_BANKS[6])
+        scatter_on_scalar(0, 2 * C, 3 * C)
         quantise(3)
+        gated_blocks(2, 1, A_BANKS[7])
         gated_experts(0, 3, 1, A_BANKS[6])
-        scatter_on_scalar(0, 640, S)
-        gated_experts(2, 2, 2, TURN_BANKS[0])
-        gated_experts(2, 0, 2, A_BANKS[6])
-        gated_experts(1, 2, 2, TURN_BANKS[0])
+        scatter_on_scalar(0, 3 * C, S)
+        gated_blocks(3, 1, A_BANKS[6])
         scatter_on_vector(1, 0, S)
-        for first, end in ((0, 384), (384, 704), (704, S)):
+        for first, end in ((704, S), (384, 704), (0, 384)):
             scatter_on_scalar(2, first, end)
-        add_and_store([nc.gpsimd] * 4, 0)
+        add_and_store([nc.gpsimd] * 2, 0, (0, 1024, 2048))
         add_and_store([nc.vector] * 4, 1)
         add_and_store([nc.vector] * 5, 2, (0, 512, 1024, 1536, 1792, 2048))

@@ -51,7 +51,6 @@ def tile_moe_res_glu_relu_kernel(
     nc = tc.nc
     with ExitStack() as ctx:
         held = ctx.enter_context(tc.tile_pool(name="held", bufs=1))
-        ring = ctx.enter_context(tc.tile_pool(name="ring", bufs=3))
         psum = ctx.enter_context(tc.psum_pool(name="psum", bufs=1))
 
         offsets = held.tile([P, S // LIST_ROWS], U16, name="offsets")
@@ -65,7 +64,8 @@ def tile_moe_res_glu_relu_kernel(
         x_tile = held.tile([P, T], I32, name="x_tile", tag="tokens")
         x_plane = held.tile([P, T], U8, name="x_plane", align_bytes=64)
         w1_tiles = [held.tile([P, half_bytes], U8, name="w1_%d" % i, align_bytes=64) for i in range(2)]
-        w3_tiles = [held.tile([P, half_bytes], U8, name="w3_%d" % i, align_bytes=64) for i in range(2)]
+        w3_tile = held.tile([P, 2 * half_bytes], U8, name="w3_tile", align_bytes=64)
+        w3_tiles = [w3_tile[:, 0:half_bytes], w3_tile[:, half_bytes : 2 * half_bytes]]
         w2_tile = held.tile([P, E * 2 * N], U8, name="w2_tile", align_bytes=64)
         gate_tile = held.tile([P, S], F32, name="gate_tile")
         xr_tiles = {}
@@ -105,13 +105,14 @@ def tile_moe_res_glu_relu_kernel(
         load_scale_rows(nc.sync, x_plane, x_scales, 1)
         load_scale_rows(nc.sync, w1_plane, w1_scales.rearrange("e s q c -> (e s) q c"), E, (0,))
         nc.sync.dma_start(out=x_tile[:], in_=x_words.rearrange("o p t r -> p (o t r)").bitcast(I32))
-        load_words(w3_words, 0, w3_tiles[0])
         load_scale_rows(nc.sync, w1_plane, w1_scales.rearrange("e s q c -> (e s) q c"), E, (1, 2, 3,))
-        load_scale_rows(nc.sync, w3_plane, w3_scales.rearrange("e s q c -> (e s) q c"), E, (0, 1, 2,))
-        load_scale_rows(nc.sync, w2_plane, w2_scales.rearrange("e s q c -> (e s) q c"), E)
+        nc.sync.dma_start(
+            out=w3_tile[:].bitcast(I32).rearrange("p (e c) -> p e c", e=E),
+            in_=w3_words.bitcast(I32).rearrange("e s p c -> p (e s) c"),
+        )
+        load_scale_rows(nc.sync, w3_plane, w3_scales.rearrange("e s q c -> (e s) q c"), E)
         load_words(w1_words, 1, w1_tiles[1])
-        load_scale_rows(nc.sync, w3_plane, w3_scales.rearrange("e s q c -> (e s) q c"), E, (3,))
-        load_words(w3_words, 1, w3_tiles[1])
+        load_scale_rows(nc.sync, w2_plane, w2_scales.rearrange("e s q c -> (e s) q c"), E)
         load_w2(0, 1)
         load_gate(0, C)
         load_w2(1, E)
@@ -167,7 +168,7 @@ def tile_moe_res_glu_relu_kernel(
             return bank[:].rearrange("s (p u d) -> s u p d", u=2, d=2)
 
         def relu(tile):
-            relus[tile] = held.tile([P, H], F32, name="relu%d" % tile)
+            relus[tile] = held.tile([P, H], F32, name="relu%d" % tile, tag="relu%d" % tile)
             nc.scalar.activation(
                 relus[tile][:].rearrange("s (u p d) -> s u p d", u=2, d=2), by_pairs(a_banks[tile]), RELU
             )
@@ -177,7 +178,7 @@ def tile_moe_res_glu_relu_kernel(
         def hidden(tile):
             e, half = divmod(tile, C // P)
             if half == 0:
-                hs[e] = ring.tile([P, 2, H], BF16, name="h")
+                hs[e] = held.tile([P, 2, H], BF16, name="h%d" % e, tag="h%d" % e)
             nc.vector.tensor_tensor(
                 hs[e][:, half, :].rearrange("s (u p d) -> s u p d", u=2, d=2),
                 by_pairs(b_banks[tile]),
@@ -247,6 +248,13 @@ def tile_moe_res_glu_relu_kernel(
                 MULT,
             )
 
+        def first_block(e, number, tag, bank=None):
+            if bank is None:
+                bank = second_layer([(0, e)], number)
+            piece = held.tile([P, C], F32, name="piece%d" % e, tag=tag, align_bytes=64)
+            nc.vector.tensor_tensor(piece[:], bank[:, 0:C], gate_tile[:, e * C : (e + 1) * C], MULT)
+            nc.scalar.activation(windows[0][:].indirect(slot_offsets(e * C, C)), piece[:], COPY)
+
         def scatter_on_scalar(block, first, end):
             nc.scalar.activation(windows[block][:].indirect(slot_offsets(first, end - first)), gated[:, block, first:end], COPY)
 
@@ -275,46 +283,43 @@ def tile_moe_res_glu_relu_kernel(
         relu(4)
         hidden(1)
         turn(0)
+        regroup(0, nc.scalar.copy)
         product_a(5)
         product_b(4)
         relu(5)
         hidden(2)
         product_a(6)
         product_b(5)
+        relu(6)
         hidden(3)
         turn(1)
         regroup(1, nc.scalar.copy)
-        relu(6)
         product_a(7)
         product_b(6)
         relu(7)
-        regroup(0, nc.vector.tensor_copy)
         hidden(4)
         product_b(7)
         quantise(0)
-        first_bank = experts_product(0, 0, 1, TURN_BANKS[0])
         hidden(5)
-        gated_experts(0, 0, 1, TURN_BANKS[0], first_bank)
-        scatter_on_scalar(0, 0, C)
+        first_bank = second_layer([(0, 0)], B_BANKS[5])
         turn(2)
         regroup(2, nc.scalar.copy)
         quantise(1)
         hidden(6)
+        first_block(0, None, "stage3", first_bank)
         hidden(7)
         turn(3)
         regroup(3, nc.scalar.copy)
-        gated_blocks(0, 1, B_BANKS[4])
-        gated_experts(0, 1, 1, B_BANKS[7])
-        scatter_on_scalar(0, C, 2 * C)
-        gated_blocks(1, 1, B_BANKS[5])
         quantise(2)
-        gated_experts(0, 2, 1, B_BANKS[6])
-        scatter_on_scalar(0, 2 * C, 3 * C)
+        gated_experts(0, 1, 2, B_BANKS[7])
+        scatter_on_scalar(0, C, 640)
+        gated_experts(1, 0, 2, B_BANKS[6])
+        gated_experts(2, 0, 2, B_BANKS[5])
+        gated_blocks(2, 1, B_BANKS[4])
         quantise(3)
-        gated_blocks(2, 1, A_BANKS[7])
         gated_experts(0, 3, 1, A_BANKS[6])
-        scatter_on_scalar(0, 3 * C, S)
-        gated_blocks(3, 1, A_BANKS[6])
+        gated_blocks(3, 1, A_BANKS[7])
+        scatter_on_scalar(0, 640, S)
         scatter_on_vector(1, 0, S)
         for first, end in ((704, S), (384, 704), (0, 384)):
             scatter_on_scalar(2, first, end)

@@ -51,6 +51,7 @@ def tile_moe_res_glu_relu_kernel(
     nc = tc.nc
     with ExitStack() as ctx:
         held = ctx.enter_context(tc.tile_pool(name="held", bufs=1))
+        early = ctx.enter_context(tc.tile_pool(name="early", bufs=1))
         psum = ctx.enter_context(tc.psum_pool(name="psum", bufs=1))
 
         offsets = held.tile([P, S // LIST_ROWS], U16, name="offsets")
@@ -67,7 +68,12 @@ def tile_moe_res_glu_relu_kernel(
         w3_tile = held.tile([P, 2 * half_bytes], U8, name="w3_tile", align_bytes=64)
         w3_tiles = [w3_tile[:, 0:half_bytes], w3_tile[:, half_bytes : 2 * half_bytes]]
         w2_tile = held.tile([P, E * 2 * N], U8, name="w2_tile", align_bytes=64)
-        gate_tile = held.tile([P, S], F32, name="gate_tile")
+        gate_tiles = [
+            early.tile([P, C], F32, name="gate0", offset=H),
+            held.tile([P, C], F32, name="gate1"),
+            held.tile([P, 2 * C], F32, name="gate23"),
+        ]
+        gates = [gate_tiles[0][:], gate_tiles[1][:], gate_tiles[2][:, 0:C], gate_tiles[2][:, C : 2 * C]]
         xr_tiles = {}
 
         def load_words(words, half, w_tile):
@@ -83,7 +89,7 @@ def tile_moe_res_glu_relu_kernel(
             )
 
         def load_gate(first, end):
-            nc.sync.dma_start(out=gate_tile[:, first:end], in_=gate[0:P, first:end])
+            nc.sync.dma_start(out=gate_tiles[first // C][:], in_=gate[0:P, first:end])
 
         def load_residual(b, tag):
             xr_tiles[b] = held.tile([P, T], F32, name="xr%d" % b, tag=tag)
@@ -113,10 +119,11 @@ def tile_moe_res_glu_relu_kernel(
         load_scale_rows(nc.sync, w3_plane, w3_scales.rearrange("e s q c -> (e s) q c"), E)
         load_words(w1_words, 1, w1_tiles[1])
         load_scale_rows(nc.sync, w2_plane, w2_scales.rearrange("e s q c -> (e s) q c"), E)
-        load_w2(0, 1)
+        load_w2(0, HALF)
         load_gate(0, C)
-        load_w2(1, E)
-        load_gate(C, S)
+        load_gate(C, 2 * C)
+        load_w2(HALF, E)
+        load_gate(2 * C, S)
 
         def slot_offsets(first, count):
             return offsets[:, first // LIST_ROWS : (first + count) // LIST_ROWS]
@@ -178,7 +185,10 @@ def tile_moe_res_glu_relu_kernel(
         def hidden(tile):
             e, half = divmod(tile, C // P)
             if half == 0:
-                hs[e] = held.tile([P, 2, H], BF16, name="h%d" % e, tag="h%d" % e)
+                if e == E - 1:
+                    hs[e] = early.tile([P, 2, H], BF16, name="h_last", offset=2 * H)
+                else:
+                    hs[e] = held.tile([P, 2, H], BF16, name="h%d" % e)
             nc.vector.tensor_tensor(
                 hs[e][:, half, :].rearrange("s (u p d) -> s u p d", u=2, d=2),
                 by_pairs(b_banks[tile]),
@@ -206,7 +216,10 @@ def tile_moe_res_glu_relu_kernel(
 
         def quantise(e):
             grouped = groups[e]
-            codes = held.tile([P, C], U32, name="hq%d" % e, align_bytes=64)
+            if e == 2:
+                codes = early.tile([P, C], U32, name="hq%d" % e, offset=0, align_bytes=64)
+            else:
+                codes = held.tile([P, C], U32, name="hq%d" % e, align_bytes=64)
             scales = held.tile([P, C], U8, name="hs%d" % e, align_bytes=64)
             nc.vector.quantize_mx(out=codes[:].bitcast(FP8X4), scales=scales[:], in_=grouped[:])
             h_codes.append(codes)
@@ -229,22 +242,13 @@ def tile_moe_res_glu_relu_kernel(
 
         gated = held.tile([P, N // P, S], F32, name="gated")
 
-        def experts_product(block, first, count, number):
-            return second_layer([(block, e) for e in range(first, first + count)], number)
-
-        def gated_experts(block, first, count, number, bank=None):
-            if bank is None:
-                bank = experts_product(block, first, count, number)
-            cols = slice(first * C, (first + count) * C)
-            nc.vector.tensor_tensor(gated[:, block, cols], bank[:, 0 : count * C], gate_tile[:, cols], MULT)
-
         def gated_blocks(e, first, number):
             bank = second_layer([(first, e), (first + 1, e)], number)
             cols = slice(e * C, (e + 1) * C)
             nc.vector.tensor_tensor(
                 gated[:, first : first + 2, cols],
                 bank[:].rearrange("p (b c) -> p b c", b=2),
-                gate_tile[:, cols].unsqueeze(1).to_broadcast([P, 2, C]),
+                gates[e].unsqueeze(1).to_broadcast([P, 2, C]),
                 MULT,
             )
 
@@ -252,7 +256,7 @@ def tile_moe_res_glu_relu_kernel(
             if bank is None:
                 bank = second_layer([(0, e)], number)
             piece = held.tile([P, C], F32, name="piece%d" % e, tag=tag, align_bytes=64)
-            nc.vector.tensor_tensor(piece[:], bank[:, 0:C], gate_tile[:, e * C : (e + 1) * C], MULT)
+            nc.vector.tensor_tensor(piece[:], bank[:, 0:C], gates[e], MULT)
             nc.scalar.activation(windows[0][:].indirect(slot_offsets(e * C, C)), piece[:], COPY)
 
         def scatter_on_scalar(block, first, end):
@@ -305,21 +309,20 @@ def tile_moe_res_glu_relu_kernel(
         turn(2)
         regroup(2, nc.scalar.copy)
         quantise(1)
+        first_block(0, None, "piece0", first_bank)
+        gated_blocks(0, 1, B_BANKS[4])
         hidden(6)
-        first_block(0, None, "stage3", first_bank)
+        first_block(1, A_BANKS[6], "piece1")
         hidden(7)
         turn(3)
-        regroup(3, nc.scalar.copy)
         quantise(2)
-        gated_experts(0, 1, 2, B_BANKS[7])
-        scatter_on_scalar(0, C, 640)
-        gated_experts(1, 0, 2, B_BANKS[6])
-        gated_experts(2, 0, 2, B_BANKS[5])
-        gated_blocks(2, 1, B_BANKS[4])
+        regroup(3, nc.vector.tensor_copy)
+        first_block(2, B_BANKS[6], "piece2")
         quantise(3)
-        gated_experts(0, 3, 1, A_BANKS[6])
-        gated_blocks(3, 1, A_BANKS[7])
-        scatter_on_scalar(0, 640, S)
+        gated_blocks(1, 1, A_BANKS[7])
+        first_block(3, B_BANKS[5], "piece3")
+        gated_blocks(2, 1, B_BANKS[7])
+        gated_blocks(3, 1, B_BANKS[4])
         scatter_on_vector(1, 0, S)
         for first, end in ((704, S), (384, 704), (0, 384)):
             scatter_on_scalar(2, first, end)

@@ -29,8 +29,8 @@ ADD = mybir.AluOpType.add
 RELU = mybir.ActivationFunctionType.Relu
 COPY = mybir.ActivationFunctionType.Copy
 
-A_BANKS = (0, 1, 2, 7, 3, 4, 0, 1)
-B_BANKS = (3, 4, 0, 1, 2, 7, 3, 4)
+A_BANKS = (0, 1, 2, 7, 0, 4, 1, 2)
+B_BANKS = (3, 4, 1, 2, 3, 7, 0, 4)
 TURN_BANKS = (5, 6)
 PIECE = 512
 
@@ -95,16 +95,17 @@ def tile_moe_res_glu_relu_kernel(
             xr_tiles[b] = held.tile([P, T], F32, name="xr%d" % b, tag=tag)
             nc.sync.dma_start(out=xr_tiles[b][:], in_=xr[b * P : (b + 1) * P, :])
 
-        nc.vector.memset(x_plane[:].bitcast(I32), 0)
-        nc.vector.memset(windows[0][:, 0:BANK].bitcast(I32), 0)
+        nc.gpsimd.memset(x_plane[:].bitcast(I32), 0)
         nc.vector.memset(w1_plane[:].bitcast(I32), 0)
+        nc.vector.memset(windows[0][:, 0:BANK].bitcast(I32), 0)
         nc.vector.memset(w3_plane[:].bitcast(I32), 0)
         nc.vector.memset(w2_plane[:].bitcast(I32), 0)
-        nc.vector.memset(windows[0][:, BANK:T].bitcast(I32), 0)
+        nc.vector.memset(windows[0][:, BANK : 2 * BANK].bitcast(I32), 0)
         make_identity(nc, ident[:])
-        zeros = windows[0][:, 0:BANK].unsqueeze(1).to_broadcast([P, T // BANK, BANK])
-        for window in windows[1:]:
-            nc.scalar.activation(window[:].rearrange("p (a c) -> p a c", c=BANK), zeros, COPY)
+        for rest in (windows[0][:, 2 * BANK : T], windows[2][:], windows[1][:]):
+            repeats = rest.shape[1] // BANK
+            zeros = windows[0][:, 0:BANK].unsqueeze(1).to_broadcast([P, repeats, BANK])
+            nc.scalar.activation(rest.rearrange("p (a c) -> p a c", c=BANK), zeros, COPY)
 
         nc.sync.dma_start(offsets[:], offs)
         load_words(w1_words, 0, w1_tiles[0])
@@ -279,17 +280,18 @@ def tile_moe_res_glu_relu_kernel(
         relu(0)
         relu(1)
         product_b(2)
-        product_b(3)
-        relu(2)
-        relu(3)
-        hidden(0)
         product_a(4)
+        relu(2)
+        product_b(3)
+        relu(3)
         relu(4)
+        hidden(0)
+        product_b(4)
         hidden(1)
         turn(0)
         regroup(0, nc.scalar.copy)
         product_a(5)
-        product_b(4)
+        product_b(6)
         relu(5)
         hidden(2)
         product_a(6)
@@ -299,10 +301,9 @@ def tile_moe_res_glu_relu_kernel(
         turn(1)
         regroup(1, nc.scalar.copy)
         product_a(7)
-        product_b(6)
+        product_b(7)
         relu(7)
         hidden(4)
-        product_b(7)
         quantise(0)
         hidden(5)
         first_bank = second_layer([(0, 0)], B_BANKS[5])

@@ -52,6 +52,7 @@ def tile_moe_res_glu_relu_kernel(
     with ExitStack() as ctx:
         held = ctx.enter_context(tc.tile_pool(name="held", bufs=1))
         early = ctx.enter_context(tc.tile_pool(name="early", bufs=1))
+        spent = ctx.enter_context(tc.tile_pool(name="spent", bufs=1))
         psum = ctx.enter_context(tc.psum_pool(name="psum", bufs=1))
 
         offsets = held.tile([P, S // LIST_ROWS], U16, name="offsets")
@@ -62,11 +63,10 @@ def tile_moe_res_glu_relu_kernel(
         windows = [held.tile([P, T], F32, name="window%d" % b) for b in range(N // P)]
 
         half_bytes = HALF * 2 * H
-        x_tile = held.tile([P, T], I32, name="x_tile", tag="tokens")
+        x_tile = spent.tile([P, T], I32, name="x_tile", offset=0)
         x_plane = held.tile([P, T], U8, name="x_plane", align_bytes=64)
         w1_tiles = [held.tile([P, half_bytes], U8, name="w1_%d" % i, align_bytes=64) for i in range(2)]
-        w3_tile = held.tile([P, 2 * half_bytes], U8, name="w3_tile", align_bytes=64)
-        w3_tiles = [w3_tile[:, 0:half_bytes], w3_tile[:, half_bytes : 2 * half_bytes]]
+        w3_tiles = [held.tile([P, half_bytes], U8, name="w3_%d" % i, align_bytes=64) for i in range(2)]
         w2_tile = held.tile([P, E * 2 * N], U8, name="w2_tile", align_bytes=64)
         gate_tiles = [
             early.tile([P, C], F32, name="gate0", offset=H),
@@ -107,18 +107,17 @@ def tile_moe_res_glu_relu_kernel(
             zeros = windows[0][:, 0:BANK].unsqueeze(1).to_broadcast([P, repeats, BANK])
             nc.scalar.activation(rest.rearrange("p (a c) -> p a c", c=BANK), zeros, COPY)
 
+        tokens = x_words.rearrange("o p t r -> p (o t r)").bitcast(I32)
         nc.sync.dma_start(offsets[:], offs)
-        load_words(w1_words, 0, w1_tiles[0])
+        nc.sync.dma_start(out=x_tile[:, 0 : T // 4], in_=tokens[:, 0 : T // 4])
         load_scale_rows(nc.sync, x_plane, x_scales, 1)
-        load_scale_rows(nc.sync, w1_plane, w1_scales.rearrange("e s q c -> (e s) q c"), E, (0,))
-        nc.sync.dma_start(out=x_tile[:], in_=x_words.rearrange("o p t r -> p (o t r)").bitcast(I32))
-        load_scale_rows(nc.sync, w1_plane, w1_scales.rearrange("e s q c -> (e s) q c"), E, (1, 2, 3,))
-        nc.sync.dma_start(
-            out=w3_tile[:].bitcast(I32).rearrange("p (e c) -> p e c", e=E),
-            in_=w3_words.bitcast(I32).rearrange("e s p c -> p (e s) c"),
-        )
+        nc.sync.dma_start(out=x_tile[:, T // 4 : T], in_=tokens[:, T // 4 : T])
+        load_words(w1_words, 0, w1_tiles[0])
+        load_scale_rows(nc.sync, w1_plane, w1_scales.rearrange("e s q c -> (e s) q c"), E)
+        load_words(w3_words, 0, w3_tiles[0])
         load_scale_rows(nc.sync, w3_plane, w3_scales.rearrange("e s q c -> (e s) q c"), E)
         load_words(w1_words, 1, w1_tiles[1])
+        load_words(w3_words, 1, w3_tiles[1])
         load_scale_rows(nc.sync, w2_plane, w2_scales.rearrange("e s q c -> (e s) q c"), E)
         load_w2(0, HALF)
         load_gate(0, C)
@@ -129,15 +128,18 @@ def tile_moe_res_glu_relu_kernel(
         def slot_offsets(first, count):
             return offsets[:, first // LIST_ROWS : (first + count) // LIST_ROWS]
 
-        slot_bytes = held.tile([P, S], U8, name="slot_bytes", align_bytes=64)
-        nc.vector.tensor_copy(slot_bytes[:], x_plane[:].indirect(offsets[:]))
+        early_bytes = held.tile([P, HALF * C], U8, name="early_bytes", align_bytes=64)
+        nc.vector.tensor_copy(early_bytes[:], x_plane[:].indirect(slot_offsets(0, HALF * C)))
         expert_words = []
         for first, count in ((0, 1), (1, 1), (2, 2)):
             part = held.tile([P, count * C], U32, name="words%d" % first, align_bytes=64)
             nc.vector.tensor_copy(part[:], x_tile[:].bitcast(U32).indirect(slot_offsets(first * C, count * C)))
             expert_words.extend(part[:, i * C : (i + 1) * C] for i in range(count))
-        expert_bytes = [slot_bytes[:, e * C : (e + 1) * C] for e in range(E)]
-        load_residual(1, "tokens")
+        late_bytes = spent.tile([P, HALF * C], U8, name="late_bytes", offset=0, align_bytes=64)
+        nc.vector.tensor_copy(late_bytes[:], x_plane[:].indirect(slot_offsets(HALF * C, HALF * C)))
+        expert_bytes = [(early_bytes, late_bytes)[e // HALF][:, (e % HALF) * C : (e % HALF + 1) * C] for e in range(E)]
+        xr_tiles[1] = spent.tile([P, T], F32, name="xr1", offset=HALF * C)
+        nc.sync.dma_start(out=xr_tiles[1][:], in_=xr[P : 2 * P, :])
         load_residual(0, "xr0")
         load_residual(2, "xr2")
 

@@ -95,13 +95,14 @@ def tile_moe_res_glu_relu_kernel(
             xr_tiles[b] = held.tile([P, T], F32, name="xr%d" % b, tag=tag)
             nc.sync.dma_start(out=xr_tiles[b][:], in_=xr[b * P : (b + 1) * P, :])
 
-        nc.gpsimd.memset(x_plane[:].bitcast(I32), 0)
-        nc.vector.memset(w1_plane[:].bitcast(I32), 0)
+        nc.vector.memset(x_plane[:].bitcast(I32), 0)
         nc.vector.memset(windows[0][:, 0:BANK].bitcast(I32), 0)
+        nc.vector.memset(w1_plane[:].bitcast(I32), 0)
         nc.vector.memset(w3_plane[:].bitcast(I32), 0)
         nc.vector.memset(w2_plane[:].bitcast(I32), 0)
         nc.vector.memset(windows[0][:, BANK : 2 * BANK].bitcast(I32), 0)
-        make_identity(nc, ident[:])
+        nc.vector.memset(ident[:], 0.0)
+        make_identity(nc, ident[:], nomemset=True)
         for rest in (windows[0][:, 2 * BANK : T], windows[2][:], windows[1][:]):
             repeats = rest.shape[1] // BANK
             zeros = windows[0][:, 0:BANK].unsqueeze(1).to_broadcast([P, repeats, BANK])

@@ -65,8 +65,11 @@ def tile_moe_res_glu_relu_kernel(
         half_bytes = HALF * 2 * H
         x_tile = spent.tile([P, T], I32, name="x_tile", offset=0)
         x_plane = held.tile([P, T], U8, name="x_plane", align_bytes=64)
-        w1_tiles = [held.tile([P, half_bytes], U8, name="w1_%d" % i, align_bytes=64) for i in range(2)]
+        w1_first = [held.tile([P, 2 * H], U8, name="w1_%d" % e, align_bytes=64) for e in range(HALF)]
+        w1_rest = held.tile([P, half_bytes], U8, name="w1_rest", align_bytes=64)
+        w1_experts = [w1_first[0][:], w1_first[1][:], w1_rest[:, 0 : 2 * H], w1_rest[:, 2 * H : 4 * H]]
         w3_tiles = [held.tile([P, half_bytes], U8, name="w3_%d" % i, align_bytes=64) for i in range(2)]
+        w3_experts = [w3_tiles[e // HALF][:, (e % HALF) * 2 * H : (e % HALF + 1) * 2 * H] for e in range(E)]
         w2_tile = held.tile([P, E * 2 * N], U8, name="w2_tile", align_bytes=64)
         gate_tiles = [
             early.tile([P, C], F32, name="gate0", offset=H),
@@ -113,11 +116,13 @@ def tile_moe_res_glu_relu_kernel(
         nc.sync.dma_start(out=x_tile[:, 0 : T // 4], in_=tokens[:, 0 : T // 4])
         load_scale_rows(nc.sync, x_plane, x_scales, 1)
         nc.sync.dma_start(out=x_tile[:, T // 4 : T], in_=tokens[:, T // 4 : T])
-        load_words(w1_words, 0, w1_tiles[0])
+        w1_rows = w1_words.bitcast(I32).rearrange("e s p c -> p (e s) c")
+        nc.sync.dma_start(out=w1_first[0][:].bitcast(I32), in_=w1_rows[:, 0, :])
         load_scale_rows(nc.sync, w1_plane, w1_scales.rearrange("e s q c -> (e s) q c"), E)
+        nc.sync.dma_start(out=w1_first[1][:].bitcast(I32), in_=w1_rows[:, 1, :])
         load_words(w3_words, 0, w3_tiles[0])
         load_scale_rows(nc.sync, w3_plane, w3_scales.rearrange("e s q c -> (e s) q c"), E)
-        load_words(w1_words, 1, w1_tiles[1])
+        load_words(w1_words, 1, w1_rest)
         load_words(w3_words, 1, w3_tiles[1])
         load_scale_rows(nc.sync, w2_plane, w2_scales.rearrange("e s q c -> (e s) q c"), E)
         load_w2(0, HALF)
@@ -152,7 +157,7 @@ def tile_moe_res_glu_relu_kernel(
         def bank_tile(number):
             return psum.tile([P, BANK], F32, name="bank%d" % number, tag="bank%d" % number)
 
-        def product(tile, w_tiles, plane, number):
+        def product(tile, w_experts, plane, number):
             e, half = divmod(tile, C // P)
             cols = slice(half * P, (half + 1) * P)
             bank = bank_tile(number)
@@ -160,7 +165,7 @@ def tile_moe_res_glu_relu_kernel(
                 out=bank[:],
                 lhsT=expert_words[e][:, cols].bitcast(FP8X4),
                 lhsT_scale=expert_bytes[e][:, cols],
-                rhs=w_tiles[e // HALF][:, (e % HALF) * 2 * H : (e % HALF + 1) * 2 * H].bitcast(FP4X4),
+                rhs=w_experts[e].bitcast(FP4X4),
                 rhs_scale=plane[:, e * H : (e + 1) * H],
                 start=True,
                 stop=True,
@@ -170,10 +175,10 @@ def tile_moe_res_glu_relu_kernel(
         a_banks = {}
 
         def product_a(tile):
-            a_banks[tile] = product(tile, w1_tiles, w1_plane, A_BANKS[tile])
+            a_banks[tile] = product(tile, w1_experts, w1_plane, A_BANKS[tile])
 
         def product_b(tile):
-            b_banks[tile] = product(tile, w3_tiles, w3_plane, B_BANKS[tile])
+            b_banks[tile] = product(tile, w3_experts, w3_plane, B_BANKS[tile])
 
         def by_pairs(bank):
             return bank[:].rearrange("s (p u d) -> s u p d", u=2, d=2)

@@ -29,10 +29,8 @@ ADD = mybir.AluOpType.add
 RELU = mybir.ActivationFunctionType.Relu
 COPY = mybir.ActivationFunctionType.Copy
 
-A_BANKS = (0, 1, 2, 7, 0, 4, 1, 2)
-B_BANKS = (3, 4, 1, 2, 3, 7, 0, 4)
-TURN_BANKS = (5, 6)
-PIECE = 512
+A_BANKS = (0, 1, 2, 7, 0, 7, 1, 3)
+B_BANKS = (3, 4, 1, 2, 3, 4, 2, 4)
 
 
 def load_scale_rows(queue, plane, scales, groups, which=range(4)):
@@ -68,15 +66,16 @@ def tile_moe_res_glu_relu_kernel(
         w1_first = [held.tile([P, 2 * H], U8, name="w1_%d" % e, align_bytes=64) for e in range(HALF)]
         w1_rest = held.tile([P, half_bytes], U8, name="w1_rest", align_bytes=64)
         w1_experts = [w1_first[0][:], w1_first[1][:], w1_rest[:, 0 : 2 * H], w1_rest[:, 2 * H : 4 * H]]
-        w3_tiles = [held.tile([P, half_bytes], U8, name="w3_%d" % i, align_bytes=64) for i in range(2)]
-        w3_experts = [w3_tiles[e // HALF][:, (e % HALF) * 2 * H : (e % HALF + 1) * 2 * H] for e in range(E)]
+        w3_first = held.tile([P, half_bytes], U8, name="w3_first", align_bytes=64)
+        w3_last = [held.tile([P, 2 * H], U8, name="w3_%d" % e, align_bytes=64) for e in range(HALF, E)]
+        w3_experts = [w3_first[:, 0 : 2 * H], w3_first[:, 2 * H : 4 * H], w3_last[0][:], w3_last[1][:]]
         w2_tile = held.tile([P, E * 2 * N], U8, name="w2_tile", align_bytes=64)
         gate_tiles = [
             early.tile([P, C], F32, name="gate0", offset=H),
-            held.tile([P, C], F32, name="gate1"),
+            held.tile([P, 2 * C], F32, name="gate01"),
             held.tile([P, 2 * C], F32, name="gate23"),
         ]
-        gates = [gate_tiles[0][:], gate_tiles[1][:], gate_tiles[2][:, 0:C], gate_tiles[2][:, C : 2 * C]]
+        gates = [gate_tiles[1 + e // HALF][:, (e % HALF) * C : (e % HALF + 1) * C] for e in range(E)]
         xr_tiles = {}
 
         def load_words(words, half, w_tile):
@@ -91,8 +90,8 @@ def tile_moe_res_glu_relu_kernel(
                 in_=w2_words.bitcast(I32).rearrange("e s p c -> p (e s) c")[:, first:end, :],
             )
 
-        def load_gate(first, end):
-            nc.sync.dma_start(out=gate_tiles[first // C][:], in_=gate[0:P, first:end])
+        def load_gate(number, block, first, end):
+            nc.sync.dma_start(out=gate_tiles[number][:], in_=gate[block * P : (block + 1) * P, first:end])
 
         def load_residual(b, tag):
             xr_tiles[b] = held.tile([P, T], F32, name="xr%d" % b, tag=tag)
@@ -120,16 +119,18 @@ def tile_moe_res_glu_relu_kernel(
         nc.sync.dma_start(out=w1_first[0][:].bitcast(I32), in_=w1_rows[:, 0, :])
         load_scale_rows(nc.sync, w1_plane, w1_scales.rearrange("e s q c -> (e s) q c"), E)
         nc.sync.dma_start(out=w1_first[1][:].bitcast(I32), in_=w1_rows[:, 1, :])
-        load_words(w3_words, 0, w3_tiles[0])
+        load_words(w3_words, 0, w3_first)
         load_scale_rows(nc.sync, w3_plane, w3_scales.rearrange("e s q c -> (e s) q c"), E)
         load_words(w1_words, 1, w1_rest)
-        load_words(w3_words, 1, w3_tiles[1])
+        w3_rows = w3_words.bitcast(I32).rearrange("e s p c -> p (e s) c")
+        nc.sync.dma_start(out=w3_last[0][:].bitcast(I32), in_=w3_rows[:, 2, :])
         load_scale_rows(nc.sync, w2_plane, w2_scales.rearrange("e s q c -> (e s) q c"), E)
         load_w2(0, HALF)
-        load_gate(0, C)
-        load_gate(C, 2 * C)
+        nc.sync.dma_start(out=w3_last[1][:].bitcast(I32), in_=w3_rows[:, 3, :])
+        load_gate(0, 0, 0, C)
+        load_gate(1, 1, 0, 2 * C)
         load_w2(HALF, E)
-        load_gate(2 * C, S)
+        load_gate(2, 0, 2 * C, S)
 
         def slot_offsets(first, count):
             return offsets[:, first // LIST_ROWS : (first + count) // LIST_ROWS]
@@ -193,25 +194,29 @@ def tile_moe_res_glu_relu_kernel(
 
         def hidden(tile):
             e, half = divmod(tile, C // P)
-            if half == 0:
+            if e == 2:
+                tag = "stage0" if half else "h4"
+                hs[tile] = held.tile([P, H], BF16, name="h%d" % tile, tag=tag, align_bytes=64)[:]
+            elif half == 0:
                 if e == E - 1:
-                    hs[e] = early.tile([P, 2, H], BF16, name="h_last", offset=2 * H)
+                    both = early.tile([P, 2, H], BF16, name="h_last", offset=2 * H)
                 else:
-                    hs[e] = held.tile([P, 2, H], BF16, name="h%d" % e)
+                    both = held.tile([P, 2, H], BF16, name="h%d" % tile)
+                hs[tile], hs[tile + 1] = both[:, 0, :], both[:, 1, :]
             nc.vector.tensor_tensor(
-                hs[e][:, half, :].rearrange("s (u p d) -> s u p d", u=2, d=2),
+                hs[tile].rearrange("s (u p d) -> s u p d", u=2, d=2),
                 by_pairs(b_banks[tile]),
                 relus[tile][:].rearrange("s (u p d) -> s u p d", u=2, d=2),
                 MULT,
             )
 
-        def turn(e):
-            turned[e] = bank_tile(TURN_BANKS[e % 2])
-            pairs = hs[e][:].bitcast(F32)
+        def turn(e, number):
+            turned[e] = bank_tile(number)
             for half in range(2):
+                pairs = hs[2 * e + half].bitcast(F32)
                 for u in range(2):
                     at = (2 * half + u) * P
-                    nc.tensor.transpose(turned[e][:, at : at + P], pairs[:, half, u * P : (u + 1) * P], ident[:])
+                    nc.tensor.transpose(turned[e][:, at : at + P], pairs[:, u * P : (u + 1) * P], ident[:])
 
         groups = {}
 
@@ -225,7 +230,7 @@ def tile_moe_res_glu_relu_kernel(
 
         def quantise(e):
             grouped = groups[e]
-            if e == 2:
+            if e == 1:
                 codes = early.tile([P, C], U32, name="hq%d" % e, offset=0, align_bytes=64)
             else:
                 codes = held.tile([P, C], U32, name="hq%d" % e, align_bytes=64)
@@ -261,11 +266,10 @@ def tile_moe_res_glu_relu_kernel(
                 MULT,
             )
 
-        def first_block(e, number, tag, bank=None):
-            if bank is None:
-                bank = second_layer([(0, e)], number)
+        def first_block(e, number, tag):
+            bank = second_layer([(0, e)], number)
             piece = held.tile([P, C], F32, name="piece%d" % e, tag=tag, align_bytes=64)
-            nc.vector.tensor_tensor(piece[:], bank[:, 0:C], gates[e], MULT)
+            nc.vector.tensor_tensor(piece[:], bank[:, 0:C], gates[e] if e else gate_tiles[0][:], MULT)
             nc.scalar.activation(windows[0][:].indirect(slot_offsets(e * C, C)), piece[:], COPY)
 
         def scatter_on_scalar(block, first, end):
@@ -283,55 +287,53 @@ def tile_moe_res_glu_relu_kernel(
 
         for tile in range(4):
             product_a(tile)
-        product_b(0)
-        product_b(1)
-        relu(0)
-        relu(1)
+        for tile in range(2):
+            product_b(tile)
+            relu(tile)
         product_b(2)
         product_a(4)
         relu(2)
         product_b(3)
         relu(3)
-        relu(4)
+        product_a(5)
         hidden(0)
         product_b(4)
+        relu(4)
         hidden(1)
-        turn(0)
-        regroup(0, nc.scalar.copy)
-        product_a(5)
-        product_b(6)
         relu(5)
+        turn(0, 5)
+        regroup(0, nc.scalar.copy)
+        product_b(5)
         hidden(2)
         product_a(6)
-        product_b(5)
         relu(6)
         hidden(3)
-        turn(1)
+        turn(1, 6)
         regroup(1, nc.scalar.copy)
-        product_a(7)
-        product_b(7)
-        relu(7)
+        product_b(6)
         hidden(4)
+        product_a(7)
+        relu(7)
         quantise(0)
         hidden(5)
-        first_bank = second_layer([(0, 0)], B_BANKS[5])
-        turn(2)
+        first_block(0, 0, "piece0")
+        product_b(7)
+        turn(2, 0)
         regroup(2, nc.scalar.copy)
         quantise(1)
-        first_block(0, None, "piece0", first_bank)
-        gated_blocks(0, 1, B_BANKS[4])
         hidden(6)
-        first_block(1, A_BANKS[6], "piece1")
         hidden(7)
-        turn(3)
+        first_block(1, 7, "piece1")
+        gated_blocks(0, 1, 2)
+        turn(3, 6)
         quantise(2)
         regroup(3, nc.vector.tensor_copy)
-        first_block(2, B_BANKS[6], "piece2")
+        first_block(2, 4, "piece2")
         quantise(3)
-        gated_blocks(1, 1, A_BANKS[7])
-        first_block(3, B_BANKS[5], "piece3")
-        gated_blocks(2, 1, B_BANKS[7])
-        gated_blocks(3, 1, B_BANKS[4])
+        gated_blocks(1, 1, 0)
+        first_block(3, 5, "piece3")
+        gated_blocks(2, 1, 7)
+        gated_blocks(3, 1, 1)
         scatter_on_vector(1, 0, S)
         for first, end in ((704, S), (384, 704), (0, 384)):
             scatter_on_scalar(2, first, end)

@@ -137,6 +137,21 @@ def tile_moe_res_glu_relu_kernel(
 
         early_bytes = held.tile([P, HALF * C], U8, name="early_bytes", align_bytes=64)
         nc.vector.tensor_copy(early_bytes[:], x_plane[:].indirect(slot_offsets(0, HALF * C)))
+        warm_words = held.tile([P, C], I32, name="warm_words", align_bytes=64)
+        warm_plane = held.tile([P, BANK], U8, name="warm_plane", align_bytes=64)
+        nc.vector.tensor_copy(warm_words[:], x_tile[:, 0:C])
+        nc.vector.tensor_copy(warm_plane[:].bitcast(I32), x_plane[:, 0:BANK].bitcast(I32))
+        for number in (5, 6):
+            warm = psum.tile([P, BANK], F32, name="warm%d" % number, tag="bank%d" % number)
+            nc.tensor.matmul_mx(
+                out=warm[:],
+                lhsT=warm_words[:, 0:P].bitcast(FP8X4),
+                lhsT_scale=warm_plane[:, 0:P],
+                rhs=warm_words[:].bitcast(U8).bitcast(FP4X4),
+                rhs_scale=warm_plane[:],
+                start=True,
+                stop=True,
+            )
         expert_words = []
         for first, count in ((0, 1), (1, 1), (2, 2)):
             part = held.tile([P, count * C], U32, name="words%d" % first, align_bytes=64)
@@ -266,6 +281,10 @@ def tile_moe_res_glu_relu_kernel(
                 MULT,
             )
 
+        def gated_block(e, block, bank, place):
+            cols = slice(e * C, (e + 1) * C)
+            nc.vector.tensor_tensor(gated[:, block, cols], bank[:, place * C : (place + 1) * C], gates[e], MULT)
+
         def first_block(e, number, tag):
             bank = second_layer([(0, e)], number)
             piece = held.tile([P, C], F32, name="piece%d" % e, tag=tag, align_bytes=64)
@@ -327,12 +346,14 @@ def tile_moe_res_glu_relu_kernel(
         gated_blocks(0, 1, 2)
         turn(3, 6)
         quantise(2)
+        second = second_layer([(1, 1), (2, 1)], 3)
+        gated_block(1, 1, second, 0)
         regroup(3, nc.vector.tensor_copy)
         first_block(2, 4, "piece2")
         quantise(3)
-        gated_blocks(1, 1, 0)
-        first_block(3, 5, "piece3")
+        gated_block(1, 2, second, 1)
         gated_blocks(2, 1, 7)
+        first_block(3, 5, "piece3")
         gated_blocks(3, 1, 1)
         scatter_on_vector(1, 0, S)
         for first, end in ((704, S), (384, 704), (0, 384)):

@@ -30,6 +30,7 @@ RELU = mybir.ActivationFunctionType.Relu
 COPY = mybir.ActivationFunctionType.Copy
 
 A_BANKS = (0, 1, 2, 7, 0, 7, 1, 3)
+EARLY = 3
 B_BANKS = (3, 4, 1, 2, 3, 4, 2, 4)
 
 
@@ -102,10 +103,9 @@ def tile_moe_res_glu_relu_kernel(
         nc.vector.memset(w1_plane[:].bitcast(I32), 0)
         nc.vector.memset(w3_plane[:].bitcast(I32), 0)
         nc.vector.memset(w2_plane[:].bitcast(I32), 0)
-        nc.vector.memset(windows[0][:, BANK : 2 * BANK].bitcast(I32), 0)
         nc.vector.memset(ident[:], 0.0)
         make_identity(nc, ident[:], nomemset=True)
-        for rest in (windows[0][:, 2 * BANK : T], windows[2][:], windows[1][:]):
+        for rest in (windows[0][:, BANK:T], windows[1][:]):
             repeats = rest.shape[1] // BANK
             zeros = windows[0][:, 0:BANK].unsqueeze(1).to_broadcast([P, repeats, BANK])
             nc.scalar.activation(rest.rearrange("p (a c) -> p a c", c=BANK), zeros, COPY)
@@ -135,8 +135,6 @@ def tile_moe_res_glu_relu_kernel(
         def slot_offsets(first, count):
             return offsets[:, first // LIST_ROWS : (first + count) // LIST_ROWS]
 
-        early_bytes = held.tile([P, HALF * C], U8, name="early_bytes", align_bytes=64)
-        nc.vector.tensor_copy(early_bytes[:], x_plane[:].indirect(slot_offsets(0, HALF * C)))
         warm_words = held.tile([P, C], I32, name="warm_words", align_bytes=64)
         warm_plane = held.tile([P, BANK], U8, name="warm_plane", align_bytes=64)
         nc.vector.tensor_copy(warm_words[:], x_tile[:, 0:C])
@@ -152,14 +150,17 @@ def tile_moe_res_glu_relu_kernel(
                 start=True,
                 stop=True,
             )
+        early_bytes = held.tile([P, EARLY * C], U8, name="early_bytes", align_bytes=64)
+        nc.vector.tensor_copy(early_bytes[:], x_plane[:].indirect(slot_offsets(0, EARLY * C)))
         expert_words = []
         for first, count in ((0, 1), (1, 1), (2, 2)):
             part = held.tile([P, count * C], U32, name="words%d" % first, align_bytes=64)
             nc.vector.tensor_copy(part[:], x_tile[:].bitcast(U32).indirect(slot_offsets(first * C, count * C)))
             expert_words.extend(part[:, i * C : (i + 1) * C] for i in range(count))
-        late_bytes = spent.tile([P, HALF * C], U8, name="late_bytes", offset=0, align_bytes=64)
-        nc.vector.tensor_copy(late_bytes[:], x_plane[:].indirect(slot_offsets(HALF * C, HALF * C)))
-        expert_bytes = [(early_bytes, late_bytes)[e // HALF][:, (e % HALF) * C : (e % HALF + 1) * C] for e in range(E)]
+        late_bytes = spent.tile([P, C], U8, name="late_bytes", offset=0, align_bytes=64)
+        nc.vector.tensor_copy(late_bytes[:], x_plane[:].indirect(slot_offsets(EARLY * C, C)))
+        expert_bytes = [early_bytes[:, e * C : (e + 1) * C] for e in range(EARLY)] + [late_bytes[:]]
+        nc.sync.dma_start(out=windows[2][:], in_=windows[1][:])
         xr_tiles[1] = spent.tile([P, T], F32, name="xr1", offset=HALF * C)
         nc.sync.dma_start(out=xr_tiles[1][:], in_=xr[P : 2 * P, :])
         load_residual(0, "xr0")
@@ -358,6 +359,6 @@ def tile_moe_res_glu_relu_kernel(
         scatter_on_vector(1, 0, S)
         for first, end in ((704, S), (384, 704), (0, 384)):
             scatter_on_scalar(2, first, end)
-        add_and_store([nc.gpsimd] * 2, 0, (0, 1024, 2048))
+        add_and_store([nc.gpsimd] * 2, 0, (0, 1408, 2048))
         add_and_store([nc.vector] * 4, 1)
         add_and_store([nc.vector] * 5, 2, (0, 512, 1024, 1536, 1792, 2048))

@@ -105,7 +105,7 @@ def tile_moe_res_glu_relu_kernel(
         nc.vector.memset(w2_plane[:].bitcast(I32), 0)
         nc.vector.memset(ident[:], 0.0)
         make_identity(nc, ident[:], nomemset=True)
-        for rest in (windows[0][:, BANK:T], windows[1][:]):
+        for rest in (windows[0][:, BANK:T], windows[2][:]):
             repeats = rest.shape[1] // BANK
             zeros = windows[0][:, 0:BANK].unsqueeze(1).to_broadcast([P, repeats, BANK])
             nc.scalar.activation(rest.rearrange("p (a c) -> p a c", c=BANK), zeros, COPY)
@@ -135,21 +135,6 @@ def tile_moe_res_glu_relu_kernel(
         def slot_offsets(first, count):
             return offsets[:, first // LIST_ROWS : (first + count) // LIST_ROWS]
 
-        warm_words = held.tile([P, C], I32, name="warm_words", align_bytes=64)
-        warm_plane = held.tile([P, BANK], U8, name="warm_plane", align_bytes=64)
-        nc.vector.tensor_copy(warm_words[:], x_tile[:, 0:C])
-        nc.vector.tensor_copy(warm_plane[:].bitcast(I32), x_plane[:, 0:BANK].bitcast(I32))
-        for number in (5, 6):
-            warm = psum.tile([P, BANK], F32, name="warm%d" % number, tag="bank%d" % number)
-            nc.tensor.matmul_mx(
-                out=warm[:],
-                lhsT=warm_words[:, 0:P].bitcast(FP8X4),
-                lhsT_scale=warm_plane[:, 0:P],
-                rhs=warm_words[:].bitcast(U8).bitcast(FP4X4),
-                rhs_scale=warm_plane[:],
-                start=True,
-                stop=True,
-            )
         early_bytes = held.tile([P, EARLY * C], U8, name="early_bytes", align_bytes=64)
         nc.vector.tensor_copy(early_bytes[:], x_plane[:].indirect(slot_offsets(0, EARLY * C)))
         expert_words = []
@@ -160,7 +145,7 @@ def tile_moe_res_glu_relu_kernel(
         late_bytes = spent.tile([P, C], U8, name="late_bytes", offset=0, align_bytes=64)
         nc.vector.tensor_copy(late_bytes[:], x_plane[:].indirect(slot_offsets(EARLY * C, C)))
         expert_bytes = [early_bytes[:, e * C : (e + 1) * C] for e in range(EARLY)] + [late_bytes[:]]
-        nc.sync.dma_start(out=windows[2][:], in_=windows[1][:])
+        nc.sync.dma_start(out=windows[1][:], in_=windows[2][:])
         xr_tiles[1] = spent.tile([P, T], F32, name="xr1", offset=HALF * C)
         nc.sync.dma_start(out=xr_tiles[1][:], in_=xr[P : 2 * P, :])
         load_residual(0, "xr0")
@@ -298,6 +283,15 @@ def tile_moe_res_glu_relu_kernel(
         def scatter_on_vector(block, first, end):
             nc.vector.tensor_copy(windows[block][:].indirect(slot_offsets(first, end - first)), gated[:, block, first:end])
 
+        def plain_result(e, block, number):
+            bank = second_layer([(block, e)], number)
+            nc.scalar.copy(gated[:, block, e * C : (e + 1) * C], bank[:, 0:C])
+
+        def gate_and_scatter(e, block):
+            nc.vector.tensor_tensor(
+                windows[block][:].indirect(slot_offsets(e * C, C)), gated[:, block, e * C : (e + 1) * C], gates[e], MULT
+            )
+
         def add_and_store(engines, block, cuts=(0, 512, 1024, 1536, 2048)):
             total = held.tile([P, T], F32, name="total%d" % block, tag="xr0" if block == 1 else "total%d" % block)
             for c in range(len(cuts) - 1):
@@ -344,21 +338,24 @@ def tile_moe_res_glu_relu_kernel(
         hidden(6)
         hidden(7)
         first_block(1, 7, "piece1")
-        gated_blocks(0, 1, 2)
+        plain_result(0, 1, 7)
+        late = second_layer([(2, 0)], 2)
+        gated_block(1, 1, second_layer([(1, 1)], 3), 0)
         turn(3, 6)
-        quantise(2)
-        second = second_layer([(1, 1), (2, 1)], 3)
-        gated_block(1, 1, second, 0)
         regroup(3, nc.vector.tensor_copy)
-        first_block(2, 4, "piece2")
+        quantise(2)
         quantise(3)
-        gated_block(1, 2, second, 1)
-        gated_blocks(2, 1, 7)
+        first_block(2, 4, "piece2")
         first_block(3, 5, "piece3")
+        gated_blocks(2, 1, 0)
         gated_blocks(3, 1, 1)
-        scatter_on_vector(1, 0, S)
-        for first, end in ((704, S), (384, 704), (0, 384)):
+        gate_and_scatter(0, 1)
+        gated_block(1, 2, second_layer([(2, 1)], 5), 0)
+        scatter_on_vector(1, C, S)
+        nc.vector.tensor_tensor(gated[:, 1, 0:C], late[:, 0:C], gates[0], MULT)
+        for first, end in ((640, S), (C, 640)):
             scatter_on_scalar(2, first, end)
+        nc.scalar.activation(windows[2][:].indirect(slot_offsets(0, C)), gated[:, 1, 0:C], COPY)
         add_and_store([nc.gpsimd] * 2, 0, (0, 1408, 2048))
         add_and_store([nc.vector] * 4, 1)
         add_and_store([nc.vector] * 5, 2, (0, 512, 1024, 1536, 1792, 2048))

@@ -11,6 +11,7 @@ LIST_ROWS = 16
 SCALE_ROWS = 16
 QUADRANT = 32
 HALF = E // 2
+FRONT = 256
 ROW = 4 * T
 
 FLOPS = 2 * S * (2 * K * H + H * N)
@@ -137,18 +138,21 @@ def tile_moe_res_glu_relu_kernel(
 
         early_bytes = held.tile([P, EARLY * C], U8, name="early_bytes", align_bytes=64)
         nc.vector.tensor_copy(early_bytes[:], x_plane[:].indirect(slot_offsets(0, EARLY * C)))
-        expert_words = []
-        for first, count in ((0, 1), (1, 1), (2, 2)):
-            part = held.tile([P, count * C], U32, name="words%d" % first, align_bytes=64)
-            nc.vector.tensor_copy(part[:], x_tile[:].bitcast(U32).indirect(slot_offsets(first * C, count * C)))
-            expert_words.extend(part[:, i * C : (i + 1) * C] for i in range(count))
+        tile_words = []
+        for first, count in ((0, 1), (1, 1), (2, 2), (4, 4)):
+            part = held.tile([P, count * P], U32, name="words%d" % first, align_bytes=64)
+            nc.vector.tensor_copy(part[:], x_tile[:].bitcast(U32).indirect(slot_offsets(first * P, count * P)))
+            tile_words.extend(part[:, i * P : (i + 1) * P] for i in range(count))
         late_bytes = spent.tile([P, C], U8, name="late_bytes", offset=0, align_bytes=64)
         nc.vector.tensor_copy(late_bytes[:], x_plane[:].indirect(slot_offsets(EARLY * C, C)))
         expert_bytes = [early_bytes[:, e * C : (e + 1) * C] for e in range(EARLY)] + [late_bytes[:]]
         nc.sync.dma_start(out=windows[1][:], in_=windows[2][:])
         xr_tiles[1] = spent.tile([P, T], F32, name="xr1", offset=HALF * C)
         nc.sync.dma_start(out=xr_tiles[1][:], in_=xr[P : 2 * P, :])
-        load_residual(0, "xr0")
+        xr_rest = held.tile([P, T - FRONT], F32, name="xr0", tag="xr0")
+        nc.sync.dma_start(out=xr_rest[:], in_=xr[0:P, FRONT:T])
+        xr_front = held.tile([P, FRONT], F32, name="xr_front")
+        nc.sync.dma_start(out=xr_front[:], in_=xr[0:P, 0:FRONT])
         load_residual(2, "xr2")
 
         h_codes, h_scales = [], []
@@ -165,7 +169,7 @@ def tile_moe_res_glu_relu_kernel(
             bank = bank_tile(number)
             nc.tensor.matmul_mx(
                 out=bank[:],
-                lhsT=expert_words[e][:, cols].bitcast(FP8X4),
+                lhsT=tile_words[tile].bitcast(FP8X4),
                 lhsT_scale=expert_bytes[e][:, cols],
                 rhs=w_experts[e].bitcast(FP4X4),
                 rhs_scale=plane[:, e * H : (e + 1) * H],
@@ -292,12 +296,14 @@ def tile_moe_res_glu_relu_kernel(
                 windows[block][:].indirect(slot_offsets(e * C, C)), gated[:, block, e * C : (e + 1) * C], gates[e], MULT
             )
 
-        def add_and_store(engines, block, cuts=(0, 512, 1024, 1536, 2048)):
-            total = held.tile([P, T], F32, name="total%d" % block, tag="xr0" if block == 1 else "total%d" % block)
-            for c in range(len(cuts) - 1):
-                cols = slice(cuts[c], cuts[c + 1])
-                engines[c].tensor_tensor(total[:, cols], windows[block][:, cols], xr_tiles[block][:, cols], ADD)
-                nc.sync.dma_start(out=out[block * P : (block + 1) * P, cols], in_=total[:, cols])
+        def add_and_store(engine, block, cols, residual, sums):
+            engine.tensor_tensor(sums, windows[block][:, cols], residual, ADD)
+            nc.sync.dma_start(out=out[block * P : (block + 1) * P, cols], in_=sums)
+
+        def add_pieces(engine, block, cuts, residual, total):
+            for first, end in zip(cuts[:-1], cuts[1:]):
+                at = slice(first - cuts[0], end - cuts[0])
+                add_and_store(engine, block, slice(first, end), residual[:, at], total[:, at])
 
         for tile in range(4):
             product_a(tile)
@@ -356,6 +362,10 @@ def tile_moe_res_glu_relu_kernel(
         for first, end in ((640, S), (C, 640)):
             scatter_on_scalar(2, first, end)
         nc.scalar.activation(windows[2][:].indirect(slot_offsets(0, C)), gated[:, 1, 0:C], COPY)
-        add_and_store([nc.gpsimd] * 2, 0, (0, 1408, 2048))
-        add_and_store([nc.vector] * 4, 1)
-        add_and_store([nc.vector] * 5, 2, (0, 512, 1024, 1536, 1792, 2048))
+        total0 = held.tile([P, T - FRONT], F32, name="total0")
+        add_pieces(nc.gpsimd, 0, (FRONT, 1536, T), xr_rest[:], total0[:])
+        total1 = held.tile([P, FRONT + T], F32, name="total1", tag="xr0")
+        add_pieces(nc.vector, 0, (0, FRONT), xr_front[:], total1[:, 0:FRONT])
+        add_pieces(nc.vector, 1, (0, 512, 1024, 1536, T), xr_tiles[1][:], total1[:, FRONT:])
+        total2 = held.tile([P, T], F32, name="total2")
+        add_pieces(nc.vector, 2, (0, 256, 768, 1280, 1792, T), xr_tiles[2][:], total2[:])

@@ -12,6 +12,7 @@ SCALE_ROWS = 16
 QUADRANT = 32
 HALF = E // 2
 FRONT = 256
+AHEAD = 3 * T // 8
 ROW = 4 * T
 
 FLOPS = 2 * S * (2 * K * H + H * N)
@@ -113,9 +114,9 @@ def tile_moe_res_glu_relu_kernel(
 
         tokens = x_words.rearrange("o p t r -> p (o t r)").bitcast(I32)
         nc.sync.dma_start(offsets[:], offs)
-        nc.sync.dma_start(out=x_tile[:, 0 : T // 4], in_=tokens[:, 0 : T // 4])
+        nc.sync.dma_start(out=x_tile[:, 0:AHEAD], in_=tokens[:, 0:AHEAD])
         load_scale_rows(nc.sync, x_plane, x_scales, 1)
-        nc.sync.dma_start(out=x_tile[:, T // 4 : T], in_=tokens[:, T // 4 : T])
+        nc.sync.dma_start(out=x_tile[:, AHEAD:T], in_=tokens[:, AHEAD:T])
         w1_rows = w1_words.bitcast(I32).rearrange("e s p c -> p (e s) c")
         nc.sync.dma_start(out=w1_first[0][:].bitcast(I32), in_=w1_rows[:, 0, :])
         load_scale_rows(nc.sync, w1_plane, w1_scales.rearrange("e s q c -> (e s) q c"), E)
@@ -363,9 +364,9 @@ def tile_moe_res_glu_relu_kernel(
             scatter_on_scalar(2, first, end)
         nc.scalar.activation(windows[2][:].indirect(slot_offsets(0, C)), gated[:, 1, 0:C], COPY)
         total0 = held.tile([P, T - FRONT], F32, name="total0")
-        add_pieces(nc.gpsimd, 0, (FRONT, 1536, T), xr_rest[:], total0[:])
+        add_pieces(nc.gpsimd, 0, (FRONT, 1472, T), xr_rest[:], total0[:])
         total1 = held.tile([P, FRONT + T], F32, name="total1", tag="xr0")
         add_pieces(nc.vector, 0, (0, FRONT), xr_front[:], total1[:, 0:FRONT])
         add_pieces(nc.vector, 1, (0, 512, 1024, 1536, T), xr_tiles[1][:], total1[:, FRONT:])
         total2 = held.tile([P, T], F32, name="total2")
-        add_pieces(nc.vector, 2, (0, 256, 768, 1280, 1792, T), xr_tiles[2][:], total2[:])
+        add_pieces(nc.vector, 2, (0, 256, 768, 1280, 1792, 1920, T), xr_tiles[2][:], total2[:])

@@ -224,6 +224,22 @@ def tile_moe_res_glu_relu_kernel(
                     at = (2 * half + u) * P
                     nc.tensor.transpose(turned[e][:, at : at + P], pairs[:, u * P : (u + 1) * P], ident[:])
 
+        def turn_half(tile, number):
+            bank = bank_tile(number)
+            pairs = hs[tile].bitcast(F32)
+            for u in range(2):
+                nc.tensor.transpose(bank[:, u * P : (u + 1) * P], pairs[:, u * P : (u + 1) * P], ident[:])
+            return bank
+
+        def regroup_half(tile, bank, copy):
+            e, half = divmod(tile, C // P)
+            if e not in groups:
+                groups[e] = held.tile([P, 4 * C], BF16, name="grouped%d" % e, tag="stage%d" % e, align_bytes=64)
+            copy(
+                groups[e][:].bitcast(F32)[:, half * C : (half + 1) * C].rearrange("p (s u) -> p s u", u=2),
+                bank[:, 0:C].rearrange("p (u s) -> p s u", u=2),
+            )
+
         groups = {}
 
         def regroup(e, copy):
@@ -339,22 +355,23 @@ def tile_moe_res_glu_relu_kernel(
         hidden(5)
         first_block(0, 0, "piece0")
         product_b(7)
-        turn(2, 0)
-        regroup(2, nc.scalar.copy)
+        regroup_half(4, turn_half(4, 0), nc.scalar.copy)
         quantise(1)
         hidden(6)
-        hidden(7)
+        sixth = turn_half(5, 2)
         first_block(1, 7, "piece1")
+        hidden(7)
+        regroup_half(5, sixth, nc.vector.tensor_copy)
         plain_result(0, 1, 7)
         late = second_layer([(2, 0)], 2)
         gated_block(1, 1, second_layer([(1, 1)], 3), 0)
         turn(3, 6)
-        regroup(3, nc.vector.tensor_copy)
         quantise(2)
-        quantise(3)
+        regroup(3, nc.vector.tensor_copy)
         first_block(2, 4, "piece2")
-        first_block(3, 5, "piece3")
+        quantise(3)
         gated_blocks(2, 1, 0)
+        first_block(3, 5, "piece3")
         gated_blocks(3, 1, 1)
         gate_and_scatter(0, 1)
         gated_block(1, 2, second_layer([(2, 1)], 5), 0)

from contextlib import ExitStack

import concourse.mybir as mybir
from concourse.masks import make_identity

K, T, E, C, H, N = 512, 2048, 4, 256, 512, 384
S = E * C
P = 128
BANK = 512
LIST_ROWS = 16
SCALE_ROWS = 16
QUADRANT = 32
HALF = E // 2
FRONT = 256
AHEAD = 3 * T // 8
ROW = 4 * T

FLOPS = 2 * S * (2 * K * H + H * N)
BYTES = K * T + K * T // 32 + E * (2 * K * H + H * N) * 17 // 32 + 4 * S + 2 * P * S // LIST_ROWS + 2 * 4 * N * T

F32 = mybir.dt.float32
BF16 = mybir.dt.bfloat16
I32 = mybir.dt.int32
U32 = mybir.dt.uint32
U16 = mybir.dt.uint16
U8 = mybir.dt.uint8
FP8X4 = mybir.dt.float8_e4m3fn_x4
FP4X4 = mybir.dt.float4_e2m1fn_x4
MULT = mybir.AluOpType.mult
ADD = mybir.AluOpType.add
RELU = mybir.ActivationFunctionType.Relu
COPY = mybir.ActivationFunctionType.Copy

A_BANKS = (0, 1, 2, 7, 0, 7, 1, 3)
EARLY = 3
B_BANKS = (3, 4, 1, 2, 3, 4, 2, 4)


def load_scale_rows(queue, plane, scales, groups, which=range(4)):
    rows = scales.bitcast(I32)
    dst = plane[:].bitcast(I32)
    for r in which:
        queue.dma_start(
            out=dst[r:P:QUADRANT, :].rearrange("q (g c) -> q g c", g=groups),
            in_=rows[:, r:SCALE_ROWS:4, :].rearrange("g q c -> q g c"),
        )


def tile_moe_res_glu_relu_kernel(
    tc, x_words, x_scales, xr, w1_words, w1_scales, w3_words, w3_scales, w2_words, w2_scales, gate, offs, out
):
    nc = tc.nc
    with ExitStack() as ctx:
        held = ctx.enter_context(tc.tile_pool(name="held", bufs=1))
        early = ctx.enter_context(tc.tile_pool(name="early", bufs=1))
        spent = ctx.enter_context(tc.tile_pool(name="spent", bufs=1))
        psum = ctx.enter_context(tc.psum_pool(name="psum", bufs=1))

        offsets = held.tile([P, S // LIST_ROWS], U16, name="offsets")
        w1_plane = held.tile([P, E * H], U8, name="w1_plane", align_bytes=64)
        w3_plane = held.tile([P, E * H], U8, name="w3_plane", align_bytes=64)
        w2_plane = held.tile([P, E * N], U8, name="w2_plane", align_bytes=64)
        ident = held.tile([P, P], F32, name="ident")
        windows = [held.tile([P, T], F32, name="window%d" % b) for b in range(N // P)]

        half_bytes = HALF * 2 * H
        x_tile = spent.tile([P, T], I32, name="x_tile", offset=0)
        x_plane = held.tile([P, T], U8, name="x_plane", align_bytes=64)
        w1_first = [held.tile([P, 2 * H], U8, name="w1_%d" % e, align_bytes=64) for e in range(HALF)]
        w1_rest = held.tile([P, half_bytes], U8, name="w1_rest", align_bytes=64)
        w1_experts = [w1_first[0][:], w1_first[1][:], w1_rest[:, 0 : 2 * H], w1_rest[:, 2 * H : 4 * H]]
        w3_first = held.tile([P, half_bytes], U8, name="w3_first", align_bytes=64)
        w3_last = [held.tile([P, 2 * H], U8, name="w3_%d" % e, align_bytes=64) for e in range(HALF, E)]
        w3_experts = [w3_first[:, 0 : 2 * H], w3_first[:, 2 * H : 4 * H], w3_last[0][:], w3_last[1][:]]
        w2_tile = held.tile([P, E * 2 * N], U8, name="w2_tile", align_bytes=64)
        gate_tiles = [
            early.tile([P, C], F32, name="gate0", offset=H),
            held.tile([P, 2 * C], F32, name="gate01"),
            held.tile([P, 2 * C], F32, name="gate23"),
        ]
        gates = [gate_tiles[1 + e // HALF][:, (e % HALF) * C : (e % HALF + 1) * C] for e in range(E)]
        xr_tiles = {}

        def load_words(words, half, w_tile):
            nc.sync.dma_start(
                out=w_tile[:].bitcast(I32).rearrange("p (e c) -> p e c", e=HALF),
                in_=words.bitcast(I32).rearrange("e s p c -> p (e s) c")[:, half * HALF : (half + 1) * HALF, :],
            )

        def load_w2(first, end):
            nc.sync.dma_start(
                out=w2_tile[:, first * 2 * N : end * 2 * N].bitcast(I32).rearrange("p (e c) -> p e c", e=end - first),
                in_=w2_words.bitcast(I32).rearrange("e s p c -> p (e s) c")[:, first:end, :],
            )

        def load_gate(number, block, first, end):
            nc.sync.dma_start(out=gate_tiles[number][:], in_=gate[block * P : (block + 1) * P, first:end])

        def load_residual(b, tag):
            xr_tiles[b] = held.tile([P, T], F32, name="xr%d" % b, tag=tag)
            nc.sync.dma_start(out=xr_tiles[b][:], in_=xr[b * P : (b + 1) * P, :])

        nc.vector.memset(x_plane[:].bitcast(I32), 0)
        nc.vector.memset(windows[0][:, 0:BANK].bitcast(I32), 0)
        nc.vector.memset(w1_plane[:].bitcast(I32), 0)
        nc.vector.memset(w3_plane[:].bitcast(I32), 0)
        nc.vector.memset(w2_plane[:].bitcast(I32), 0)
        nc.vector.memset(ident[:], 0.0)
        make_identity(nc, ident[:], nomemset=True)
        for rest in (windows[0][:, BANK:T], windows[2][:]):
            repeats = rest.shape[1] // BANK
            zeros = windows[0][:, 0:BANK].unsqueeze(1).to_broadcast([P, repeats, BANK])
            nc.scalar.activation(rest.rearrange("p (a c) -> p a c", c=BANK), zeros, COPY)

        tokens = x_words.rearrange("o p t r -> p (o t r)").bitcast(I32)
        nc.sync.dma_start(offsets[:], offs)
        nc.sync.dma_start(out=x_tile[:, 0:AHEAD], in_=tokens[:, 0:AHEAD])
        load_scale_rows(nc.sync, x_plane, x_scales, 1)
        nc.sync.dma_start(out=x_tile[:, AHEAD:T], in_=tokens[:, AHEAD:T])
        w1_rows = w1_words.bitcast(I32).rearrange("e s p c -> p (e s) c")
        nc.sync.dma_start(out=w1_first[0][:].bitcast(I32), in_=w1_rows[:, 0, :])
        load_scale_rows(nc.sync, w1_plane, w1_scales.rearrange("e s q c -> (e s) q c"), E)
        nc.sync.dma_start(out=w1_first[1][:].bitcast(I32), in_=w1_rows[:, 1, :])
        load_words(w3_words, 0, w3_first)
        load_scale_rows(nc.sync, w3_plane, w3_scales.rearrange("e s q c -> (e s) q c"), E)
        load_words(w1_words, 1, w1_rest)
        w3_rows = w3_words.bitcast(I32).rearrange("e s p c -> p (e s) c")
        nc.sync.dma_start(out=w3_last[0][:].bitcast(I32), in_=w3_rows[:, 2, :])
        load_scale_rows(nc.sync, w2_plane, w2_scales.rearrange("e s q c -> (e s) q c"), E)
        load_w2(0, HALF)
        nc.sync.dma_start(out=w3_last[1][:].bitcast(I32), in_=w3_rows[:, 3, :])
        load_gate(0, 0, 0, C)
        load_gate(1, 1, 0, 2 * C)
        load_w2(HALF, E)
        load_gate(2, 0, 2 * C, S)

        def slot_offsets(first, count):
            return offsets[:, first // LIST_ROWS : (first + count) // LIST_ROWS]

        early_bytes = held.tile([P, EARLY * C], U8, name="early_bytes", align_bytes=64)
        nc.vector.tensor_copy(early_bytes[:], x_plane[:].indirect(slot_offsets(0, EARLY * C)))
        tile_words = []
        for first, count in ((0, 1), (1, 1), (2, 2), (4, 4)):
            part = held.tile([P, count * P], U32, name="words%d" % first, align_bytes=64)
            nc.vector.tensor_copy(part[:], x_tile[:].bitcast(U32).indirect(slot_offsets(first * P, count * P)))
            tile_words.extend(part[:, i * P : (i + 1) * P] for i in range(count))
        late_bytes = spent.tile([P, C], U8, name="late_bytes", offset=0, align_bytes=64)
        nc.vector.tensor_copy(late_bytes[:], x_plane[:].indirect(slot_offsets(EARLY * C, C)))
        expert_bytes = [early_bytes[:, e * C : (e + 1) * C] for e in range(EARLY)] + [late_bytes[:]]
        nc.sync.dma_start(out=windows[1][:], in_=windows[2][:])
        xr_tiles[1] = spent.tile([P, T], F32, name="xr1", offset=HALF * C)
        nc.sync.dma_start(out=xr_tiles[1][:], in_=xr[P : 2 * P, :])
        xr_rest = held.tile([P, T - FRONT], F32, name="xr0", tag="xr0")
        nc.sync.dma_start(out=xr_rest[:], in_=xr[0:P, FRONT:T])
        xr_front = held.tile([P, FRONT], F32, name="xr_front")
        nc.sync.dma_start(out=xr_front[:], in_=xr[0:P, 0:FRONT])
        load_residual(2, "xr2")

        h_codes, h_scales = [], []
        turned = {}
        relus = {}
        b_banks = {}

        def bank_tile(number):
            return psum.tile([P, BANK], F32, name="bank%d" % number, tag="bank%d" % number)

        def product(tile, w_experts, plane, number):
            e, half = divmod(tile, C // P)
            cols = slice(half * P, (half + 1) * P)
            bank = bank_tile(number)
            nc.tensor.matmul_mx(
                out=bank[:],
                lhsT=tile_words[tile].bitcast(FP8X4),
                lhsT_scale=expert_bytes[e][:, cols],
                rhs=w_experts[e].bitcast(FP4X4),
                rhs_scale=plane[:, e * H : (e + 1) * H],
                start=True,
                stop=True,
            )
            return bank

        a_banks = {}

        def product_a(tile):
            a_banks[tile] = product(tile, w1_experts, w1_plane, A_BANKS[tile])

        def product_b(tile):
            b_banks[tile] = product(tile, w3_experts, w3_plane, B_BANKS[tile])

        def by_pairs(bank):
            return bank[:].rearrange("s (p u d) -> s u p d", u=2, d=2)

        def relu(tile):
            relus[tile] = held.tile([P, H], F32, name="relu%d" % tile, tag="relu%d" % tile)
            nc.scalar.activation(
                relus[tile][:].rearrange("s (u p d) -> s u p d", u=2, d=2), by_pairs(a_banks[tile]), RELU
            )

        hs = {}

        def hidden(tile):
            e, half = divmod(tile, C // P)
            if e == 2:
                tag = "stage0" if half else "h4"
                hs[tile] = held.tile([P, H], BF16, name="h%d" % tile, tag=tag, align_bytes=64)[:]
            elif half == 0:
                if e == E - 1:
                    both = early.tile([P, 2, H], BF16, name="h_last", offset=2 * H)
                else:
                    both = held.tile([P, 2, H], BF16, name="h%d" % tile)
                hs[tile], hs[tile + 1] = both[:, 0, :], both[:, 1, :]
            nc.vector.tensor_tensor(
                hs[tile].rearrange("s (u p d) -> s u p d", u=2, d=2),
                by_pairs(b_banks[tile]),
                relus[tile][:].rearrange("s (u p d) -> s u p d", u=2, d=2),
                MULT,
            )

        def turn(e, number):
            turned[e] = bank_tile(number)
            for half in range(2):
                pairs = hs[2 * e + half].bitcast(F32)
                for u in range(2):
                    at = (2 * half + u) * P
                    nc.tensor.transpose(turned[e][:, at : at + P], pairs[:, u * P : (u + 1) * P], ident[:])

        def turn_half(tile, number):
            bank = bank_tile(number)
            pairs = hs[tile].bitcast(F32)
            for u in range(2):
                nc.tensor.transpose(bank[:, u * P : (u + 1) * P], pairs[:, u * P : (u + 1) * P], ident[:])
            return bank

        def regroup_half(tile, bank, copy):
            e, half = divmod(tile, C // P)
            if e not in groups:
                groups[e] = held.tile([P, 4 * C], BF16, name="grouped%d" % e, tag="stage%d" % e, align_bytes=64)
            copy(
                groups[e][:].bitcast(F32)[:, half * C : (half + 1) * C].rearrange("p (s u) -> p s u", u=2),
                bank[:, 0:C].rearrange("p (u s) -> p s u", u=2),
            )

        groups = {}

        def regroup(e, copy):
            grouped = held.tile([P, 4 * C], BF16, name="grouped%d" % e, tag="stage%d" % e, align_bytes=64)
            groups[e] = grouped
            copy(
                grouped[:].bitcast(F32).rearrange("p (f s u) -> p f s u", f=2, u=2),
                turned[e][:].rearrange("p (f u s) -> p f s u", f=2, u=2),
            )

        def quantise(e):
            grouped = groups[e]
            if e == 1:
                codes = early.tile([P, C], U32, name="hq%d" % e, offset=0, align_bytes=64)
            else:
                codes = held.tile([P, C], U32, name="hq%d" % e, align_bytes=64)
            scales = held.tile([P, C], U8, name="hs%d" % e, align_bytes=64)
            nc.vector.quantize_mx(out=codes[:].bitcast(FP8X4), scales=scales[:], in_=grouped[:])
            h_codes.append(codes)
            h_scales.append(scales)

        def second_layer(units, number):
            bank = bank_tile(number)
            for place, (block, e) in enumerate(units):
                col = e * N + block * P
                nc.tensor.matmul_mx(
                    out=bank[:, place * C : (place + 1) * C],
                    lhsT=w2_tile[:, 2 * col : 2 * (col + P)].bitcast(FP4X4),
                    lhsT_scale=w2_plane[:, col : col + P],
                    rhs=h_codes[e][:].bitcast(FP8X4),
                    rhs_scale=h_scales[e][:],
                    start=True,
                    stop=True,
                )
            return bank

        gated = held.tile([P, N // P, S], F32, name="gated")

        def gated_blocks(e, first, number):
            bank = second_layer([(first, e), (first + 1, e)], number)
            cols = slice(e * C, (e + 1) * C)
            nc.vector.tensor_tensor(
                gated[:, first : first + 2, cols],
                bank[:].rearrange("p (b c) -> p b c", b=2),
                gates[e].unsqueeze(1).to_broadcast([P, 2, C]),
                MULT,
            )

        def gated_block(e, block, bank, place):
            cols = slice(e * C, (e + 1) * C)
            nc.vector.tensor_tensor(gated[:, block, cols], bank[:, place * C : (place + 1) * C], gates[e], MULT)

        def first_block(e, number, tag):
            bank = second_layer([(0, e)], number)
            piece = held.tile([P, C], F32, name="piece%d" % e, tag=tag, align_bytes=64)
            nc.vector.tensor_tensor(piece[:], bank[:, 0:C], gates[e] if e else gate_tiles[0][:], MULT)
            nc.scalar.activation(windows[0][:].indirect(slot_offsets(e * C, C)), piece[:], COPY)

        def scatter_on_scalar(block, first, end):
            nc.scalar.activation(windows[block][:].indirect(slot_offsets(first, end - first)), gated[:, block, first:end], COPY)

        def scatter_on_vector(block, first, end):
            nc.vector.tensor_copy(windows[block][:].indirect(slot_offsets(first, end - first)), gated[:, block, first:end])

        def plain_result(e, block, number):
            bank = second_layer([(block, e)], number)
            nc.scalar.copy(gated[:, block, e * C : (e + 1) * C], bank[:, 0:C])

        def gate_and_scatter(e, block):
            nc.vector.tensor_tensor(
                windows[block][:].indirect(slot_offsets(e * C, C)), gated[:, block, e * C : (e + 1) * C], gates[e], MULT
            )

        def add_and_store(engine, block, cols, residual, sums):
            engine.tensor_tensor(sums, windows[block][:, cols], residual, ADD)
            nc.sync.dma_start(out=out[block * P : (block + 1) * P, cols], in_=sums)

        def add_pieces(engine, block, cuts, residual, total):
            for first, end in zip(cuts[:-1], cuts[1:]):
                at = slice(first - cuts[0], end - cuts[0])
                add_and_store(engine, block, slice(first, end), residual[:, at], total[:, at])

        for tile in range(4):
            product_a(tile)
        for tile in range(2):
            product_b(tile)
            relu(tile)
        product_b(2)
        product_a(4)
        relu(2)
        product_b(3)
        relu(3)
        product_a(5)
        hidden(0)
        product_b(4)
        relu(4)
        hidden(1)
        relu(5)
        turn(0, 5)
        regroup(0, nc.scalar.copy)
        product_b(5)
        hidden(2)
        product_a(6)
        relu(6)
        hidden(3)
        turn(1, 6)
        regroup(1, nc.scalar.copy)
        product_b(6)
        hidden(4)
        product_a(7)
        relu(7)
        quantise(0)
        hidden(5)
        first_block(0, 0, "piece0")
        product_b(7)
        regroup_half(4, turn_half(4, 0), nc.scalar.copy)
        quantise(1)
        hidden(6)
        sixth = turn_half(5, 2)
        first_block(1, 7, "piece1")
        hidden(7)
        regroup_half(5, sixth, nc.vector.tensor_copy)
        plain_result(0, 1, 7)
        late = second_layer([(2, 0)], 2)
        gated_block(1, 1, second_layer([(1, 1)], 3), 0)
        turn(3, 6)
        quantise(2)
        regroup(3, nc.vector.tensor_copy)
        first_block(2, 4, "piece2")
        quantise(3)
        gated_blocks(2, 1, 0)
        first_block(3, 5, "piece3")
        gated_blocks(3, 1, 1)
        gate_and_scatter(0, 1)
        gated_block(1, 2, second_layer([(2, 1)], 5), 0)
        scatter_on_vector(1, C, S)
        nc.vector.tensor_tensor(gated[:, 1, 0:C], late[:, 0:C], gates[0], MULT)
        for first, end in ((640, S), (C, 640)):
            scatter_on_scalar(2, first, end)
        nc.scalar.activation(windows[2][:].indirect(slot_offsets(0, C)), gated[:, 1, 0:C], COPY)
        total0 = held.tile([P, T - FRONT], F32, name="total0")
        add_pieces(nc.gpsimd, 0, (FRONT, 1472, T), xr_rest[:], total0[:])
        total1 = held.tile([P, FRONT + T], F32, name="total1", tag="xr0")
        add_pieces(nc.vector, 0, (0, FRONT), xr_front[:], total1[:, 0:FRONT])
        add_pieces(nc.vector, 1, (0, 512, 1024, 1536, T), xr_tiles[1][:], total1[:, FRONT:])
        total2 = held.tile([P, T], F32, name="total2")
        add_pieces(nc.vector, 2, (0, 256, 768, 1280, 1792, 1920, T), xr_tiles[2][:], total2[:])
